import numpy as np
import ml_dtypes


def mxq(x, axis, fmt="e4m3"):
    dtype, down = {"e4m3": (ml_dtypes.float8_e4m3fn, 7), "e5m2": (ml_dtypes.float8_e5m2, 14)}[fmt]
    v = np.moveaxis(np.asarray(x, np.float32).astype(ml_dtypes.bfloat16).astype(np.float64), axis, -1)
    blocks = v.reshape(v.shape[:-1] + (-1, 32))
    amax = np.abs(blocks).max(-1, keepdims=True)
    byte = np.maximum(np.where(amax > 0, np.frexp(amax)[1] - 1 + 127, 0) - down, 1)
    scale = np.exp2(byte - 127.0)
    codes = (blocks / scale).astype(np.float32).astype(dtype).astype(np.float64)
    return np.moveaxis((codes * scale).reshape(v.shape), -1, axis)


WIDE = False


def mx_kscale(k):
    if not WIDE:
        return np.ones(k)
    levels = np.array([10, -10, 5, -5, 0])
    if k % 512:
        return np.exp2(np.random.permutation(np.resize(levels, k // 32))).repeat(32)
    a = np.empty((k // 512, 16))
    for p in range(k // 512):
        a[p, :8] = np.random.permutation(np.resize(levels, 8))
        for g in range(8):
            far = levels[np.abs(levels - a[p, g]) >= 10]
            a[p, g + 8] = far[np.random.randint(len(far))]
    return np.exp2(a.ravel()).repeat(32)


def f64(x):
    return np.asarray(x).astype(np.float64)


def striped(idx):
    return np.tile(idx.reshape(-1, 16).T, (8, 1)).astype(np.uint16)


def unstriped(offs):
    return offs[:16].T.reshape(-1).astype(np.int64)


def pack_weight(w):
    k, n = w.shape
    w = f64(np.asarray(w, np.float32).astype(ml_dtypes.bfloat16)).reshape(k // 32, 32, n)
    amax = np.abs(w).max(1)
    byte = np.clip(np.where(amax > 0, np.frexp(amax)[1] - 1 + 127 - 7, 1), 1, 254)
    scaled = (w * np.exp2(127.0 - byte)[:, None, :]).reshape(k, n).astype(np.float32)
    words = np.ascontiguousarray(scaled.reshape(k // 512, 128, 4, n).transpose(0, 1, 3, 2)).astype(ml_dtypes.float8_e4m3fn).view(np.uint8)
    return words, np.ascontiguousarray(byte.astype(np.uint8).reshape(k // 512, 16, n))


def unpack_weight(words, scales):
    g, p, n, _ = words.shape
    vals = np.ascontiguousarray(words).view(ml_dtypes.float8_e4m3fn).astype(np.float64) * np.repeat(np.exp2(scales.astype(np.float64) - 127.0), 8, axis=1)[..., None]
    return vals.transpose(0, 1, 3, 2).reshape(g * 512, n)


K, T, S, H, N = 512, 4096, 1024, 512, 128


def setup_inputs():
    n = np.random.standard_normal
    s = mx_kscale(K)[:, None]
    u = mx_kscale(H)
    packed_xT = pack_weight(n((K, T)) * s)
    return {
        "x_words": packed_xT[0],
        "x_scales": packed_xT[1],
        "w1": (n((K, H)) / np.sqrt(K) / s).astype(np.float32),
        "w2": (n((H, N)) / np.sqrt(H) / u[:, None]).astype(np.float32),
        "gamma": (np.random.uniform(0.5, 1.5, (H, 1)) * u[:, None]).astype(np.float32),
        "offs": striped(np.random.permutation(T)[:S]),
    }


def reference(x_words, x_scales, w1, w2, gamma, offs):
    xq = unpack_weight(x_words, x_scales)[:, unstriped(offs)]
    h = mxq(f64(w1), 0, "e4m3").T @ xq
    hn = (h - h.mean(axis=1, keepdims=True)) / np.sqrt(h.var(axis=1, keepdims=True) + 1e-5)
    z = f64(gamma) * hn
    return mxq(f64(w2), 0, "e4m3").T @ mxq(z, 0, "e4m3")

@@ -1,0 +1,148 @@
+from contextlib import ExitStack
+
+import concourse.mybir as mybir
+
+K, T, S, H, N = 512, 4096, 1024, 512, 128
+FLOPS = 2 * K * H * S + 2 * H * N * S
+EPS = 1e-5
+
+F32 = mybir.dt.float32
+BF16 = mybir.dt.bfloat16
+I32 = mybir.dt.int32
+U32 = mybir.dt.uint32
+U16 = mybir.dt.uint16
+U8 = mybir.dt.uint8
+FP8X4 = mybir.dt.float8_e4m3fn_x4
+ACT = mybir.ActivationFunctionType
+ALU = mybir.AluOpType
+
+P = 128
+PACK = 4
+BANK = 512
+ROW0 = 112
+
+
+def tile_picked_inorm_none_p_kernel(tc, x_words, x_scales, w1, w2, gamma, offs, out):
+    nc = tc.nc
+    halves = S // BANK
+    with ExitStack() as ctx:
+        keep = ctx.enter_context(tc.tile_pool(name="keep", bufs=1))
+        psum = ctx.enter_context(tc.psum_pool(name="psum", bufs=1))
+
+        offsets = keep.tile([P, S // 16], U16, name="offsets")
+        table_words = keep.tile([P, T], U32, name="table_words", align_bytes=64)
+        table_scales = keep.tile([P, T], U8, name="table_scales", align_bytes=64)
+        w1_raw = [keep.tile([P, PACK, H // 2], F32, name=f"w1_raw{c}") for c in range(2)]
+        w2_raw = keep.tile([P, PACK, N], F32, name="w2_raw")
+        gain = keep.tile([P, PACK], F32, name="gain")
+
+        x_codes = keep.tile([P, S], U32, name="x_codes", align_bytes=64)
+        picked_scales = keep.tile([P, S], U8, name="picked_scales", align_bytes=64)
+        x_plane = keep.tile([P, S], U8, name="x_plane", align_bytes=64)
+
+        nc.vector.memset(table_scales[0:ROW0, :].bitcast(I32), 0)
+        nc.vector.memset(x_plane[:].bitcast(I32), 0)
+        nc.sync.dma_start(table_scales[ROW0:P, :].bitcast(I32), x_scales[0].bitcast(I32))
+        nc.sync.dma_start(offsets[:], offs)
+        nc.sync.dma_start(gain[:], gamma.rearrange("(p t) o -> p (t o)", t=PACK))
+        nc.sync.dma_start(table_words[:].bitcast(I32), x_words[0].rearrange("p n t -> p (n t)").bitcast(I32))
+        w1_rows = w1.rearrange("(p j) c -> p j c", j=PACK)
+        for c in range(2):
+            nc.sync.dma_start(w1_raw[c][:], w1_rows[:, :, c * (H // 2) : (c + 1) * (H // 2)])
+        nc.sync.dma_start(w2_raw[:], w2.rearrange("(p t) n -> p t n", t=PACK))
+
+        warm = keep.tile([P, 1], F32, name="warm")
+        warm_out = keep.tile([P, 1], F32, name="warm_out")
+        nc.gpsimd.memset(warm[:], 1.0)
+        nc.scalar.activation(warm_out[:], warm[:], ACT.Abs_reciprocal_sqrt)
+
+        nc.vector.tensor_copy(picked_scales[:], table_scales[:].indirect(offsets[:]))
+        for q in range(4):
+            nc.scalar.dma_start(x_plane[32 * q : 32 * q + 4, :].bitcast(I32), picked_scales[ROW0 + 4 * q : ROW0 + 4 * q + 4, :].bitcast(I32))
+        nc.vector.tensor_copy(x_codes[:], table_words[:].indirect(offsets[:]))
+
+        w1_bf = keep.tile([P, PACK, P, PACK], BF16, name="w1_bf", align_bytes=64)
+
+        def deal_w1(copy, c, m0, m1):
+            src = w1_raw[c][:].rearrange("p j (m t) -> p m j t", t=PACK)[:, m0:m1]
+            dst = w1_bf[:].rearrange("p t m j -> p m j t")[:, 64 * c + m0 : 64 * c + m1]
+            copy(dst, src)
+
+        deal_w1(nc.scalar.copy, 0, 0, 64)
+        deal_w1(nc.scalar.copy, 1, 0, 20)
+        deal_w1(nc.vector.tensor_copy, 1, 20, 64)
+
+        w1_codes = [keep.tile([P, P], U32, name=f"w1_codes{t}", align_bytes=64) for t in range(PACK)]
+        w1_plane = [keep.tile([P, P], U8, name=f"w1_plane{t}", align_bytes=64) for t in range(PACK)]
+        for t in range(PACK):
+            nc.vector.quantize_mx(out=w1_codes[t][:].bitcast(FP8X4), scales=w1_plane[t][:], in_=w1_bf[:, t].rearrange("p m j -> p (m j)"))
+
+        w2_bf = keep.tile([P, N, PACK], BF16, name="w2_bf", align_bytes=64)
+        w2_codes = keep.tile([P, N], U32, name="w2_codes", align_bytes=64)
+        w2_plane = keep.tile([P, N], U8, name="w2_plane", align_bytes=64)
+        nc.scalar.copy(w2_bf[:].rearrange("p (c i) t -> p c t i", i=4), w2_raw[:].rearrange("p t (c i) -> p c t i", i=4))
+        nc.vector.quantize_mx(out=w2_codes[:].bitcast(FP8X4), scales=w2_plane[:], in_=w2_bf[:].rearrange("p n t -> p (n t)"))
+
+        factors = [keep.tile([P, 2], F32, name=f"factors{t}") for t in range(PACK)]
+        for t in range(PACK):
+            nc.vector.tensor_copy(factors[t][:, 0:1], gain[:, t : t + 1])
+
+        z_rows = [keep.tile([P, PACK, BANK], BF16, name=f"z_rows{s}", align_bytes=64) for s in range(halves)]
+        h = {}
+        affine = {}
+
+        def normalise_on_scalar(t, s):
+            nc.scalar.activation(z_rows[s][:, t, :], h[t, s][:], ACT.Identity, bias=affine[t][:, 1:2], scale=affine[t][:, 0:1])
+
+        for t in range(PACK):
+            stats = keep.tile([P, halves, 6], F32, name=f"stats{t}")
+            for s in range(halves):
+                h[t, s] = psum.tile([P, BANK], F32, name=f"h{t}_{s}", tag=f"bank{halves * t + s}")
+                cols = slice(s * BANK, (s + 1) * BANK)
+                nc.tensor.matmul_mx(
+                    out=h[t, s][:],
+                    lhsT=w1_codes[t][:].bitcast(FP8X4),
+                    lhsT_scale=w1_plane[t][:],
+                    rhs=x_codes[:, cols].bitcast(FP8X4),
+                    rhs_scale=x_plane[:, cols],
+                    start=True,
+                    stop=True,
+                )
+                nc.vector.bn_stats(stats[:, s, :], h[t, s][:])
+            moments = keep.tile([P, 2], F32, name=f"moments{t}")
+            nc.vector.bn_aggr(moments[:], stats[:].rearrange("p s e -> p (s e)"))
+            nc.vector.tensor_scalar(factors[t][:, 1:2], moments[:, 0:1], gain[:, t : t + 1], -1.0, ALU.mult, ALU.mult)
+            rstd = keep.tile([P, 1], F32, name=f"rstd{t}")
+            nc.scalar.activation(rstd[:], moments[:, 1:2], ACT.Abs_reciprocal_sqrt, bias=EPS)
+            affine[t] = keep.tile([P, 2], F32, name=f"affine{t}")
+            nc.scalar.activation(affine[t][:], factors[t][:], ACT.Identity, scale=rstd[:])
+            if t > 0:
+                for s in range(halves):
+                    normalise_on_scalar(t - 1, s)
+        last = PACK - 1
+        for c0 in (0, 256):
+            nc.vector.tensor_scalar(z_rows[0][:, last, c0 : c0 + 256], h[last, 0][:, c0 : c0 + 256], affine[last][:, 0:1], affine[last][:, 1:2], ALU.mult, ALU.add)
+        normalise_on_scalar(last, 1)
+
+        chunks = [(0, 256, nc.vector.tensor_copy), (256, 256, nc.vector.tensor_copy), (512, 256, nc.scalar.copy), (768, 128, nc.scalar.copy), (896, 128, nc.vector.tensor_copy)]
+        z_bf = []
+        for c, (first, width, copy) in enumerate(chunks):
+            s, c0 = divmod(first, BANK)
+            z_bf.append(keep.tile([P, width, PACK], BF16, name=f"z_bf{c}", align_bytes=64))
+            copy(z_bf[c][:].rearrange("p (c i) t -> p c t i", i=4), z_rows[s][:, :, c0 : c0 + width].rearrange("p t (c i) -> p c t i", i=4))
+            z_codes = keep.tile([P, width], U32, name=f"z_codes{c}", align_bytes=64)
+            z_plane = keep.tile([P, width], U8, name=f"z_plane{c}", align_bytes=64)
+            nc.vector.quantize_mx(out=z_codes[:].bitcast(FP8X4), scales=z_plane[:], in_=z_bf[c][:].rearrange("p n t -> p (n t)"))
+            y = psum.tile([P, width], F32, name=f"y{c}", tag=f"bank{c}")
+            nc.tensor.matmul_mx(
+                out=y[:],
+                lhsT=w2_codes[:].bitcast(FP8X4),
+                lhsT_scale=w2_plane[:],
+                rhs=z_codes[:].bitcast(FP8X4),
+                rhs_scale=z_plane[:],
+                start=True,
+                stop=True,
+            )
+            result = keep.tile([P, width], F32, name=f"result{c}")
+            nc.scalar.copy(result[:], y[:])
+            nc.sync.dma_start(out[:, first : first + width], result[:])

@@ -20,6 +20,7 @@ P = 128
 PACK = 4
 BANK = 512
 ROW0 = 112
+RUN = 256
 
 
 def tile_picked_inorm_none_p_kernel(tc, x_words, x_scales, w1, w2, gamma, offs, out):
@@ -35,8 +36,7 @@ def tile_picked_inorm_none_p_kernel(tc, x_words, x_scales, w1, w2, gamma, offs, 
         w1_raw = [keep.tile([P, PACK, H // 2], F32, name=f"w1_raw{c}") for c in range(2)]
         w2_raw = keep.tile([P, PACK, N], F32, name="w2_raw")
         gain = keep.tile([P, PACK], F32, name="gain")
-
-        x_codes = keep.tile([P, S], U32, name="x_codes", align_bytes=64)
+        x_codes = [keep.tile([P, BANK], U32, name=f"x_codes{s}", align_bytes=64) for s in range(halves)]
         picked_scales = keep.tile([P, S], U8, name="picked_scales", align_bytes=64)
         x_plane = keep.tile([P, S], U8, name="x_plane", align_bytes=64)
 
@@ -44,92 +44,140 @@ def tile_picked_inorm_none_p_kernel(tc, x_words, x_scales, w1, w2, gamma, offs, 
         nc.vector.memset(x_plane[:].bitcast(I32), 0)
         nc.sync.dma_start(table_scales[ROW0:P, :].bitcast(I32), x_scales[0].bitcast(I32))
         nc.sync.dma_start(offsets[:], offs)
-        nc.sync.dma_start(gain[:], gamma.rearrange("(p t) o -> p (t o)", t=PACK))
         nc.sync.dma_start(table_words[:].bitcast(I32), x_words[0].rearrange("p n t -> p (n t)").bitcast(I32))
         w1_rows = w1.rearrange("(p j) c -> p j c", j=PACK)
         for c in range(2):
             nc.sync.dma_start(w1_raw[c][:], w1_rows[:, :, c * (H // 2) : (c + 1) * (H // 2)])
         nc.sync.dma_start(w2_raw[:], w2.rearrange("(p t) n -> p t n", t=PACK))
+        nc.gpsimd.dma_start(gain[:], gamma.rearrange("(p t) o -> p (t o)", t=PACK))
 
         warm = keep.tile([P, 1], F32, name="warm")
         warm_out = keep.tile([P, 1], F32, name="warm_out")
         nc.gpsimd.memset(warm[:], 1.0)
         nc.scalar.activation(warm_out[:], warm[:], ACT.Abs_reciprocal_sqrt)
 
+        factors = keep.tile([P, PACK, 2], F32, name="factors")
+        minus_gain = keep.tile([P, PACK], F32, name="minus_gain")
+        nc.gpsimd.tensor_copy(factors[:, :, 0], gain[:])
+        nc.gpsimd.tensor_scalar(minus_gain[:], gain[:], -1.0, 0.0, ALU.mult, ALU.add)
+        stats = [keep.tile([P, halves, 2, 3], F32, name=f"stats{t}") for t in range(PACK)]
+        nc.vector.memset(stats[1][:, 0, :, 0], float(RUN))
+
         nc.vector.tensor_copy(picked_scales[:], table_scales[:].indirect(offsets[:]))
         for q in range(4):
             nc.scalar.dma_start(x_plane[32 * q : 32 * q + 4, :].bitcast(I32), picked_scales[ROW0 + 4 * q : ROW0 + 4 * q + 4, :].bitcast(I32))
-        nc.vector.tensor_copy(x_codes[:], table_words[:].indirect(offsets[:]))
+        for s in range(halves):
+            nc.vector.tensor_copy(x_codes[s][:], table_words[:].indirect(offsets[:, s * BANK // 16 : (s + 1) * BANK // 16]))
+
+        h = {}
+        for t in range(PACK):
+            for s in range(halves):
+                h[t, s] = psum.tile([P, BANK], F32, name=f"h{t}_{s}", tag=f"bank{halves * t + s}")
 
         w1_bf = keep.tile([P, PACK, P, PACK], BF16, name="w1_bf", align_bytes=64)
 
-        def deal_w1(copy, c, m0, m1):
-            src = w1_raw[c][:].rearrange("p j (m t) -> p m j t", t=PACK)[:, m0:m1]
-            dst = w1_bf[:].rearrange("p t m j -> p m j t")[:, 64 * c + m0 : 64 * c + m1]
+        def deal_w1(copy, c, t0, t1):
+            src = w1_raw[c][:].rearrange("p j (m t) -> p m j t", t=PACK)[:, :, :, t0:t1]
+            dst = w1_bf[:].rearrange("p t m j -> p m j t")[:, 64 * c : 64 * (c + 1), :, t0:t1]
             copy(dst, src)
 
-        deal_w1(nc.scalar.copy, 0, 0, 64)
-        deal_w1(nc.scalar.copy, 1, 0, 20)
-        deal_w1(nc.vector.tensor_copy, 1, 20, 64)
+        deal_w1(nc.scalar.copy, 0, 0, 4)
+        deal_w1(nc.vector.tensor_copy, 1, 0, 1)
+        deal_w1(nc.vector.tensor_copy, 1, 1, 2)
+        deal_w1(nc.scalar.copy, 1, 2, 4)
 
         w1_codes = [keep.tile([P, P], U32, name=f"w1_codes{t}", align_bytes=64) for t in range(PACK)]
         w1_plane = [keep.tile([P, P], U8, name=f"w1_plane{t}", align_bytes=64) for t in range(PACK)]
         for t in range(PACK):
             nc.vector.quantize_mx(out=w1_codes[t][:].bitcast(FP8X4), scales=w1_plane[t][:], in_=w1_bf[:, t].rearrange("p m j -> p (m j)"))
 
+        z_rows = [keep.tile([P, PACK, BANK], BF16, name=f"z_rows{s}", align_bytes=64) for s in range(halves)]
+        affine = {}
+
+        def product(t, s):
+            nc.tensor.matmul_mx(
+                out=h[t, s][:],
+                lhsT=w1_codes[t][:].bitcast(FP8X4),
+                lhsT_scale=w1_plane[t][:],
+                rhs=x_codes[s][:].bitcast(FP8X4),
+                rhs_scale=x_plane[:, s * BANK : (s + 1) * BANK],
+                start=True,
+                stop=True,
+            )
+
+        def stats_on_vector(t, s):
+            nc.vector.bn_stats(stats[t][:, s].rearrange("p r e -> p (r e)"), h[t, s][:])
+
+        def stats_on_scalar(t, s):
+            spent = keep.tile([P, BANK], BF16, name="spent")
+            for r in range(2):
+                cols = slice(r * RUN, (r + 1) * RUN)
+                nc.scalar.activation(spent[:, cols], h[t, s][:, cols], ACT.Identity, scale=1.0 / RUN, accum_out=stats[t][:, s, r, 1:2])
+            for r in range(2):
+                cols = slice(r * RUN, (r + 1) * RUN)
+                nc.scalar.activation(spent[:, cols], h[t, s][:, cols], ACT.Square, scale=-1.0, bias=stats[t][:, s, r, 1:2], accum_out=stats[t][:, s, r, 2:3])
+
+        def factors_of(t):
+            moments = keep.tile([P, 2], F32, name=f"moments{t}")
+            nc.vector.bn_aggr(moments[:], stats[t][:].rearrange("p s r e -> p (s r e)"))
+            rstd = keep.tile([P, 1], F32, name=f"rstd{t}")
+            nc.scalar.activation(rstd[:], moments[:, 1:2], ACT.Abs_reciprocal_sqrt, bias=EPS)
+            nc.scalar.activation(factors[:, t, 1:2], moments[:, 0:1], ACT.Identity, scale=minus_gain[:, t : t + 1])
+            affine[t] = keep.tile([P, 2], F32, name=f"affine{t}")
+            nc.scalar.activation(affine[t][:], factors[:, t, :], ACT.Identity, scale=rstd[:])
+
+        def normalise_on_scalar(t, s, c0=0, c1=BANK):
+            nc.scalar.activation(z_rows[s][:, t, c0:c1], h[t, s][:, c0:c1], ACT.Identity, bias=affine[t][:, 1:2], scale=affine[t][:, 0:1])
+
+        def normalise_on_vector(t, s, c0=0, c1=BANK):
+            nc.vector.tensor_scalar(z_rows[s][:, t, c0:c1], h[t, s][:, c0:c1], affine[t][:, 0:1], affine[t][:, 1:2], ALU.mult, ALU.add)
+
+        product(0, 0)
+        product(1, 0)
+        product(0, 1)
+        product(1, 1)
+        for t in (2, 3):
+            for s in range(halves):
+                product(t, s)
+        stats_on_scalar(1, 0)
+        stats_on_vector(0, 0)
+        stats_on_vector(0, 1)
+        factors_of(0)
+        stats_on_vector(1, 1)
+        factors_of(1)
+        for t in (2, 3):
+            for s in range(halves):
+                stats_on_vector(t, s)
+            factors_of(t)
         w2_bf = keep.tile([P, N, PACK], BF16, name="w2_bf", align_bytes=64)
         w2_codes = keep.tile([P, N], U32, name="w2_codes", align_bytes=64)
         w2_plane = keep.tile([P, N], U8, name="w2_plane", align_bytes=64)
         nc.scalar.copy(w2_bf[:].rearrange("p (c i) t -> p c t i", i=4), w2_raw[:].rearrange("p t (c i) -> p c t i", i=4))
         nc.vector.quantize_mx(out=w2_codes[:].bitcast(FP8X4), scales=w2_plane[:], in_=w2_bf[:].rearrange("p n t -> p (n t)"))
-
-        factors = [keep.tile([P, 2], F32, name=f"factors{t}") for t in range(PACK)]
-        for t in range(PACK):
-            nc.vector.tensor_copy(factors[t][:, 0:1], gain[:, t : t + 1])
-
-        z_rows = [keep.tile([P, PACK, BANK], BF16, name=f"z_rows{s}", align_bytes=64) for s in range(halves)]
-        h = {}
-        affine = {}
-
-        def normalise_on_scalar(t, s):
-            nc.scalar.activation(z_rows[s][:, t, :], h[t, s][:], ACT.Identity, bias=affine[t][:, 1:2], scale=affine[t][:, 0:1])
-
-        for t in range(PACK):
-            stats = keep.tile([P, halves, 6], F32, name=f"stats{t}")
+        for t in (0, 1):
             for s in range(halves):
-                h[t, s] = psum.tile([P, BANK], F32, name=f"h{t}_{s}", tag=f"bank{halves * t + s}")
-                cols = slice(s * BANK, (s + 1) * BANK)
-                nc.tensor.matmul_mx(
-                    out=h[t, s][:],
-                    lhsT=w1_codes[t][:].bitcast(FP8X4),
-                    lhsT_scale=w1_plane[t][:],
-                    rhs=x_codes[:, cols].bitcast(FP8X4),
-                    rhs_scale=x_plane[:, cols],
-                    start=True,
-                    stop=True,
-                )
-                nc.vector.bn_stats(stats[:, s, :], h[t, s][:])
-            moments = keep.tile([P, 2], F32, name=f"moments{t}")
-            nc.vector.bn_aggr(moments[:], stats[:].rearrange("p s e -> p (s e)"))
-            nc.vector.tensor_scalar(factors[t][:, 1:2], moments[:, 0:1], gain[:, t : t + 1], -1.0, ALU.mult, ALU.mult)
-            rstd = keep.tile([P, 1], F32, name=f"rstd{t}")
-            nc.scalar.activation(rstd[:], moments[:, 1:2], ACT.Abs_reciprocal_sqrt, bias=EPS)
-            affine[t] = keep.tile([P, 2], F32, name=f"affine{t}")
-            nc.scalar.activation(affine[t][:], factors[t][:], ACT.Identity, scale=rstd[:])
-            if t > 0:
-                for s in range(halves):
-                    normalise_on_scalar(t - 1, s)
-        last = PACK - 1
-        for c0 in (0, 256):
-            nc.vector.tensor_scalar(z_rows[0][:, last, c0 : c0 + 256], h[last, 0][:, c0 : c0 + 256], affine[last][:, 0:1], affine[last][:, 1:2], ALU.mult, ALU.add)
-        normalise_on_scalar(last, 1)
+                normalise_on_scalar(t, s)
+        normalise_on_vector(2, 0)
+        normalise_on_scalar(2, 1)
+        normalise_on_vector(3, 0, 0, 256)
+        normalise_on_vector(3, 0, 256, 512)
+        normalise_on_scalar(3, 1)
 
-        chunks = [(0, 256, nc.vector.tensor_copy), (256, 256, nc.vector.tensor_copy), (512, 256, nc.scalar.copy), (768, 128, nc.scalar.copy), (896, 128, nc.vector.tensor_copy)]
-        z_bf = []
-        for c, (first, width, copy) in enumerate(chunks):
-            s, c0 = divmod(first, BANK)
-            z_bf.append(keep.tile([P, width, PACK], BF16, name=f"z_bf{c}", align_bytes=64))
-            copy(z_bf[c][:].rearrange("p (c i) t -> p c t i", i=4), z_rows[s][:, :, c0 : c0 + width].rearrange("p t (c i) -> p c t i", i=4))
+
+        chunks = [(0, 256), (256, 256), (512, 256), (768, 128), (896, 128)]
+        z_bf = [keep.tile([P, width, PACK], BF16, name=f"z_bf{c}", align_bytes=64) for c, (first, width) in enumerate(chunks)]
+
+        def weave(copy, c, a, b):
+            s, c0 = divmod(chunks[c][0], BANK)
+            copy(z_bf[c][:, a:b, :].rearrange("p (c i) t -> p c t i", i=4), z_rows[s][:, :, c0 + a : c0 + b].rearrange("p t (c i) -> p c t i", i=4))
+
+        weave(nc.vector.tensor_copy, 0, 0, 256)
+        weave(nc.vector.tensor_copy, 1, 0, 256)
+        weave(nc.scalar.copy, 2, 0, 256)
+        weave(nc.scalar.copy, 3, 0, 128)
+        weave(nc.scalar.copy, 4, 0, 64)
+        weave(nc.vector.tensor_copy, 4, 64, 128)
+        for c, (first, width) in enumerate(chunks):
             z_codes = keep.tile([P, width], U32, name=f"z_codes{c}", align_bytes=64)
             z_plane = keep.tile([P, width], U8, name=f"z_plane{c}", align_bytes=64)
             nc.vector.quantize_mx(out=z_codes[:].bitcast(FP8X4), scales=z_plane[:], in_=z_bf[c][:].rearrange("p n t -> p (n t)"))
@@ -144,5 +192,6 @@ def tile_picked_inorm_none_p_kernel(tc, x_words, x_scales, w1, w2, gamma, offs, 
                 stop=True,
             )
             result = keep.tile([P, width], F32, name=f"result{c}")
-            nc.scalar.copy(result[:], y[:])
+            drain = nc.vector.tensor_copy if c == len(chunks) - 1 else nc.scalar.copy
+            drain(result[:], y[:])
             nc.sync.dma_start(out[:, first : first + width], result[:])

@@ -18,36 +18,42 @@ ALU = mybir.AluOpType
 
 P = 128
 PACK = 4
+QUADRANT = 32
+GROUP = 16
 BANK = 512
-ROW0 = 112
-RUN = 256
+HALVES = S // BANK
+SCALE_ROW0 = P - K // 32
+RUN = BANK // 2
+NEIGHBOURS = 4
+CHUNKS = ((0, 256), (256, 256), (512, 256), (768, 128), (896, 128))
+SCALAR_TAIL = 64
 
 
 def tile_picked_inorm_none_p_kernel(tc, x_words, x_scales, w1, w2, gamma, offs, out):
     nc = tc.nc
-    halves = S // BANK
     with ExitStack() as ctx:
         keep = ctx.enter_context(tc.tile_pool(name="keep", bufs=1))
         psum = ctx.enter_context(tc.psum_pool(name="psum", bufs=1))
 
-        offsets = keep.tile([P, S // 16], U16, name="offsets")
+        offsets = keep.tile([P, S // GROUP], U16, name="offsets")
         table_words = keep.tile([P, T], U32, name="table_words", align_bytes=64)
         table_scales = keep.tile([P, T], U8, name="table_scales", align_bytes=64)
-        w1_raw = [keep.tile([P, PACK, H // 2], F32, name=f"w1_raw{c}") for c in range(2)]
+        w1_raw = [keep.tile([P, 2, H], F32, name=f"w1_raw{c}") for c in range(2)]
         w2_raw = keep.tile([P, PACK, N], F32, name="w2_raw")
         gain = keep.tile([P, PACK], F32, name="gain")
-        x_codes = [keep.tile([P, BANK], U32, name=f"x_codes{s}", align_bytes=64) for s in range(halves)]
+        x_codes = [keep.tile([P, BANK], U32, name=f"x_codes{s}", align_bytes=64) for s in range(HALVES)]
         picked_scales = keep.tile([P, S], U8, name="picked_scales", align_bytes=64)
         x_plane = keep.tile([P, S], U8, name="x_plane", align_bytes=64)
 
-        nc.vector.memset(table_scales[0:ROW0, :].bitcast(I32), 0)
+        nc.vector.memset(table_scales[0:SCALE_ROW0, :].bitcast(I32), 0)
         nc.vector.memset(x_plane[:].bitcast(I32), 0)
-        nc.sync.dma_start(table_scales[ROW0:P, :].bitcast(I32), x_scales[0].bitcast(I32))
+
+        nc.sync.dma_start(table_scales[SCALE_ROW0:P, :].bitcast(I32), x_scales[0].bitcast(I32))
         nc.sync.dma_start(offsets[:], offs)
         nc.sync.dma_start(table_words[:].bitcast(I32), x_words[0].rearrange("p n t -> p (n t)").bitcast(I32))
         w1_rows = w1.rearrange("(p j) c -> p j c", j=PACK)
         for c in range(2):
-            nc.sync.dma_start(w1_raw[c][:], w1_rows[:, :, c * (H // 2) : (c + 1) * (H // 2)])
+            nc.sync.dma_start(w1_raw[c][:], w1_rows[:, 2 * c : 2 * c + 2, :])
         nc.sync.dma_start(w2_raw[:], w2.rearrange("(p t) n -> p t n", t=PACK))
         nc.gpsimd.dma_start(gain[:], gamma.rearrange("(p t) o -> p (t o)", t=PACK))
 
@@ -60,28 +66,32 @@ def tile_picked_inorm_none_p_kernel(tc, x_words, x_scales, w1, w2, gamma, offs, 
         minus_gain = keep.tile([P, PACK], F32, name="minus_gain")
         nc.gpsimd.tensor_copy(factors[:, :, 0], gain[:])
         nc.gpsimd.tensor_scalar(minus_gain[:], gain[:], -1.0, 0.0, ALU.mult, ALU.add)
-        stats = [keep.tile([P, halves, 2, 3], F32, name=f"stats{t}") for t in range(PACK)]
+        stats = [keep.tile([P, HALVES, 2, 3], F32, name=f"stats{t}") for t in range(PACK)]
         nc.vector.memset(stats[1][:, 0, :, 0], float(RUN))
 
         nc.vector.tensor_copy(picked_scales[:], table_scales[:].indirect(offsets[:]))
-        for q in range(4):
-            nc.scalar.dma_start(x_plane[32 * q : 32 * q + 4, :].bitcast(I32), picked_scales[ROW0 + 4 * q : ROW0 + 4 * q + 4, :].bitcast(I32))
-        for s in range(halves):
-            nc.vector.tensor_copy(x_codes[s][:], table_words[:].indirect(offsets[:, s * BANK // 16 : (s + 1) * BANK // 16]))
+        for q in range(P // QUADRANT):
+            nc.scalar.dma_start(
+                x_plane[QUADRANT * q : QUADRANT * q + 4, :].bitcast(I32),
+                picked_scales[SCALE_ROW0 + 4 * q : SCALE_ROW0 + 4 * q + 4, :].bitcast(I32),
+            )
+        for s in range(HALVES):
+            nc.vector.tensor_copy(x_codes[s][:], table_words[:].indirect(offsets[:, s * BANK // GROUP : (s + 1) * BANK // GROUP]))
 
         h = {}
         for t in range(PACK):
-            for s in range(halves):
-                h[t, s] = psum.tile([P, BANK], F32, name=f"h{t}_{s}", tag=f"bank{halves * t + s}")
+            for s in range(HALVES):
+                h[t, s] = psum.tile([P, BANK], F32, name=f"h{t}_{s}", tag=f"bank{HALVES * t + s}")
 
         w1_bf = keep.tile([P, PACK, P, PACK], BF16, name="w1_bf", align_bytes=64)
 
         def deal_w1(copy, c, t0, t1):
-            src = w1_raw[c][:].rearrange("p j (m t) -> p m j t", t=PACK)[:, :, :, t0:t1]
-            dst = w1_bf[:].rearrange("p t m j -> p m j t")[:, 64 * c : 64 * (c + 1), :, t0:t1]
+            src = w1_raw[c][:].rearrange("p e (m t) -> p m e t", t=PACK)[:, :, :, t0:t1]
+            dst = w1_bf[:].rearrange("p t m j -> p m j t")[:, :, 2 * c : 2 * c + 2, t0:t1]
             copy(dst, src)
 
-        deal_w1(nc.scalar.copy, 0, 0, 4)
+        deal_w1(nc.scalar.copy, 0, 0, 2)
+        deal_w1(nc.scalar.copy, 0, 2, 4)
         deal_w1(nc.vector.tensor_copy, 1, 0, 1)
         deal_w1(nc.vector.tensor_copy, 1, 1, 2)
         deal_w1(nc.scalar.copy, 1, 2, 4)
@@ -91,7 +101,7 @@ def tile_picked_inorm_none_p_kernel(tc, x_words, x_scales, w1, w2, gamma, offs, 
         for t in range(PACK):
             nc.vector.quantize_mx(out=w1_codes[t][:].bitcast(FP8X4), scales=w1_plane[t][:], in_=w1_bf[:, t].rearrange("p m j -> p (m j)"))
 
-        z_rows = [keep.tile([P, PACK, BANK], BF16, name=f"z_rows{s}", align_bytes=64) for s in range(halves)]
+        z_rows = [keep.tile([P, PACK, BANK], BF16, name=f"z_rows{s}", align_bytes=64) for s in range(HALVES)]
         affine = {}
 
         def product(t, s):
@@ -117,7 +127,7 @@ def tile_picked_inorm_none_p_kernel(tc, x_words, x_scales, w1, w2, gamma, offs, 
                 cols = slice(r * RUN, (r + 1) * RUN)
                 nc.scalar.activation(spent[:, cols], h[t, s][:, cols], ACT.Square, scale=-1.0, bias=stats[t][:, s, r, 1:2], accum_out=stats[t][:, s, r, 2:3])
 
-        def factors_of(t):
+        def affine_of(t):
             moments = keep.tile([P, 2], F32, name=f"moments{t}")
             nc.vector.bn_aggr(moments[:], stats[t][:].rearrange("p s r e -> p (s r e)"))
             rstd = keep.tile([P, 1], F32, name=f"rstd{t}")
@@ -126,58 +136,54 @@ def tile_picked_inorm_none_p_kernel(tc, x_words, x_scales, w1, w2, gamma, offs, 
             affine[t] = keep.tile([P, 2], F32, name=f"affine{t}")
             nc.scalar.activation(affine[t][:], factors[:, t, :], ACT.Identity, scale=rstd[:])
 
-        def normalise_on_scalar(t, s, c0=0, c1=BANK):
-            nc.scalar.activation(z_rows[s][:, t, c0:c1], h[t, s][:, c0:c1], ACT.Identity, bias=affine[t][:, 1:2], scale=affine[t][:, 0:1])
+        def normalise_on_scalar(t, s):
+            nc.scalar.activation(z_rows[s][:, t, :], h[t, s][:], ACT.Identity, bias=affine[t][:, 1:2], scale=affine[t][:, 0:1])
 
-        def normalise_on_vector(t, s, c0=0, c1=BANK):
+        def normalise_on_vector(t, s, c0, c1):
             nc.vector.tensor_scalar(z_rows[s][:, t, c0:c1], h[t, s][:, c0:c1], affine[t][:, 0:1], affine[t][:, 1:2], ALU.mult, ALU.add)
 
-        product(0, 0)
-        product(1, 0)
-        product(0, 1)
-        product(1, 1)
-        for t in (2, 3):
-            for s in range(halves):
-                product(t, s)
+        for pair in ((0, 1), (2,), (3,)):
+            for s in range(HALVES):
+                for t in pair:
+                    product(t, s)
         stats_on_scalar(1, 0)
-        stats_on_vector(0, 0)
-        stats_on_vector(0, 1)
-        factors_of(0)
-        stats_on_vector(1, 1)
-        factors_of(1)
-        for t in (2, 3):
-            for s in range(halves):
-                stats_on_vector(t, s)
-            factors_of(t)
+        for t in range(PACK):
+            for s in range(HALVES):
+                if (t, s) != (1, 0):
+                    stats_on_vector(t, s)
+            affine_of(t)
+
         w2_bf = keep.tile([P, N, PACK], BF16, name="w2_bf", align_bytes=64)
         w2_codes = keep.tile([P, N], U32, name="w2_codes", align_bytes=64)
         w2_plane = keep.tile([P, N], U8, name="w2_plane", align_bytes=64)
-        nc.scalar.copy(w2_bf[:].rearrange("p (c i) t -> p c t i", i=4), w2_raw[:].rearrange("p t (c i) -> p c t i", i=4))
+        nc.scalar.copy(w2_bf[:].rearrange("p (c i) t -> p c t i", i=NEIGHBOURS), w2_raw[:].rearrange("p t (c i) -> p c t i", i=NEIGHBOURS))
         nc.vector.quantize_mx(out=w2_codes[:].bitcast(FP8X4), scales=w2_plane[:], in_=w2_bf[:].rearrange("p n t -> p (n t)"))
+
         for t in (0, 1):
-            for s in range(halves):
+            for s in range(HALVES):
                 normalise_on_scalar(t, s)
-        normalise_on_vector(2, 0)
+        normalise_on_vector(2, 0, 0, BANK)
         normalise_on_scalar(2, 1)
-        normalise_on_vector(3, 0, 0, 256)
-        normalise_on_vector(3, 0, 256, 512)
+        for first, width in CHUNKS[:2]:
+            normalise_on_vector(3, 0, first, first + width)
         normalise_on_scalar(3, 1)
 
+        z_bf = [keep.tile([P, width, PACK], BF16, name=f"z_bf{c}", align_bytes=64) for c, (first, width) in enumerate(CHUNKS)]
 
-        chunks = [(0, 256), (256, 256), (512, 256), (768, 128), (896, 128)]
-        z_bf = [keep.tile([P, width, PACK], BF16, name=f"z_bf{c}", align_bytes=64) for c, (first, width) in enumerate(chunks)]
+        def weave(copy, c, n0, n1):
+            s, c0 = divmod(CHUNKS[c][0], BANK)
+            copy(
+                z_bf[c][:, n0:n1, :].rearrange("p (c i) t -> p c t i", i=NEIGHBOURS),
+                z_rows[s][:, :, c0 + n0 : c0 + n1].rearrange("p t (c i) -> p c t i", i=NEIGHBOURS),
+            )
 
-        def weave(copy, c, a, b):
-            s, c0 = divmod(chunks[c][0], BANK)
-            copy(z_bf[c][:, a:b, :].rearrange("p (c i) t -> p c t i", i=4), z_rows[s][:, :, c0 + a : c0 + b].rearrange("p t (c i) -> p c t i", i=4))
+        last = len(CHUNKS) - 1
+        for c, (first, width) in enumerate(CHUNKS[:last]):
+            weave(nc.vector.tensor_copy if first < BANK else nc.scalar.copy, c, 0, width)
+        weave(nc.scalar.copy, last, 0, SCALAR_TAIL)
+        weave(nc.vector.tensor_copy, last, SCALAR_TAIL, CHUNKS[last][1])
 
-        weave(nc.vector.tensor_copy, 0, 0, 256)
-        weave(nc.vector.tensor_copy, 1, 0, 256)
-        weave(nc.scalar.copy, 2, 0, 256)
-        weave(nc.scalar.copy, 3, 0, 128)
-        weave(nc.scalar.copy, 4, 0, 64)
-        weave(nc.vector.tensor_copy, 4, 64, 128)
-        for c, (first, width) in enumerate(chunks):
+        for c, (first, width) in enumerate(CHUNKS):
             z_codes = keep.tile([P, width], U32, name=f"z_codes{c}", align_bytes=64)
             z_plane = keep.tile([P, width], U8, name=f"z_plane{c}", align_bytes=64)
             nc.vector.quantize_mx(out=z_codes[:].bitcast(FP8X4), scales=z_plane[:], in_=z_bf[c][:].rearrange("p n t -> p (n t)"))
@@ -192,6 +198,6 @@ def tile_picked_inorm_none_p_kernel(tc, x_words, x_scales, w1, w2, gamma, offs, 
                 stop=True,
             )
             result = keep.tile([P, width], F32, name=f"result{c}")
-            drain = nc.vector.tensor_copy if c == len(chunks) - 1 else nc.scalar.copy
+            drain = nc.vector.tensor_copy if c == last else nc.scalar.copy
             drain(result[:], y[:])
             nc.sync.dma_start(out[:, first : first + width], result[:])

@@ -37,9 +37,8 @@ def tile_picked_inorm_none_p_kernel(tc, x_words, x_scales, w1, w2, gamma, offs, 
 
         offsets = keep.tile([P, S // GROUP], U16, name="offsets")
         table_words = keep.tile([P, T], U32, name="table_words", align_bytes=64)
-        table_scales = keep.tile([P, T], U8, name="table_scales", align_bytes=64)
-        w1_raw = [keep.tile([P, 2, H], F32, name=f"w1_raw{c}") for c in range(2)]
-        w2_raw = keep.tile([P, PACK, N], F32, name="w2_raw")
+        table_scales = keep.tile([P, T], U8, name="table_scales", tag="scales_then_weights", align_bytes=64)
+        w1_first = keep.tile([P, 2, H], F32, name="w1_first")
         gain = keep.tile([P, PACK], F32, name="gain")
         x_codes = [keep.tile([P, BANK], U32, name=f"x_codes{s}", align_bytes=64) for s in range(HALVES)]
         picked_scales = keep.tile([P, S], U8, name="picked_scales", align_bytes=64)
@@ -52,9 +51,7 @@ def tile_picked_inorm_none_p_kernel(tc, x_words, x_scales, w1, w2, gamma, offs, 
         nc.sync.dma_start(offsets[:], offs)
         nc.sync.dma_start(table_words[:].bitcast(I32), x_words[0].rearrange("p n t -> p (n t)").bitcast(I32))
         w1_rows = w1.rearrange("(p j) c -> p j c", j=PACK)
-        for c in range(2):
-            nc.sync.dma_start(w1_raw[c][:], w1_rows[:, 2 * c : 2 * c + 2, :])
-        nc.sync.dma_start(w2_raw[:], w2.rearrange("(p t) n -> p t n", t=PACK))
+        nc.sync.dma_start(w1_first[:], w1_rows[:, 0:2, :])
         nc.gpsimd.dma_start(gain[:], gamma.rearrange("(p t) o -> p (t o)", t=PACK))
 
         warm = keep.tile([P, 1], F32, name="warm")
@@ -71,10 +68,15 @@ def tile_picked_inorm_none_p_kernel(tc, x_words, x_scales, w1, w2, gamma, offs, 
 
         nc.vector.tensor_copy(picked_scales[:], table_scales[:].indirect(offsets[:]))
         for q in range(P // QUADRANT):
-            nc.scalar.dma_start(
+            nc.sync.dma_start(
                 x_plane[QUADRANT * q : QUADRANT * q + 4, :].bitcast(I32),
                 picked_scales[SCALE_ROW0 + 4 * q : SCALE_ROW0 + 4 * q + 4, :].bitcast(I32),
             )
+        late_weights = keep.tile([P, 2 * H + PACK * N], F32, name="late_weights", tag="scales_then_weights", align_bytes=64)
+        w1_raw = [w1_first[:], late_weights[:, 0 : 2 * H].rearrange("p (e c) -> p e c", e=2)]
+        w2_raw = late_weights[:, 2 * H :].rearrange("p (t n) -> p t n", t=PACK)
+        nc.sync.dma_start(w1_raw[1], w1_rows[:, 2:4, :])
+        nc.sync.dma_start(w2_raw, w2.rearrange("(p t) n -> p t n", t=PACK))
         for s in range(HALVES):
             nc.vector.tensor_copy(x_codes[s][:], table_words[:].indirect(offsets[:, s * BANK // GROUP : (s + 1) * BANK // GROUP]))
 
@@ -86,7 +88,7 @@ def tile_picked_inorm_none_p_kernel(tc, x_words, x_scales, w1, w2, gamma, offs, 
         w1_bf = keep.tile([P, PACK, P, PACK], BF16, name="w1_bf", align_bytes=64)
 
         def deal_w1(copy, c, t0, t1):
-            src = w1_raw[c][:].rearrange("p e (m t) -> p m e t", t=PACK)[:, :, :, t0:t1]
+            src = w1_raw[c].rearrange("p e (m t) -> p m e t", t=PACK)[:, :, :, t0:t1]
             dst = w1_bf[:].rearrange("p t m j -> p m j t")[:, :, 2 * c : 2 * c + 2, t0:t1]
             copy(dst, src)
 
@@ -156,7 +158,7 @@ def tile_picked_inorm_none_p_kernel(tc, x_words, x_scales, w1, w2, gamma, offs, 
         w2_bf = keep.tile([P, N, PACK], BF16, name="w2_bf", align_bytes=64)
         w2_codes = keep.tile([P, N], U32, name="w2_codes", align_bytes=64)
         w2_plane = keep.tile([P, N], U8, name="w2_plane", align_bytes=64)
-        nc.scalar.copy(w2_bf[:].rearrange("p (c i) t -> p c t i", i=NEIGHBOURS), w2_raw[:].rearrange("p t (c i) -> p c t i", i=NEIGHBOURS))
+        nc.scalar.copy(w2_bf[:].rearrange("p (c i) t -> p c t i", i=NEIGHBOURS), w2_raw.rearrange("p t (c i) -> p c t i", i=NEIGHBOURS))
         nc.vector.quantize_mx(out=w2_codes[:].bitcast(FP8X4), scales=w2_plane[:], in_=w2_bf[:].rearrange("p n t -> p (n t)"))
 
         for t in (0, 1):

@@ -85,6 +85,17 @@ def tile_picked_inorm_none_p_kernel(tc, x_words, x_scales, w1, w2, gamma, offs, 
             for s in range(HALVES):
                 h[t, s] = psum.tile([P, BANK], F32, name=f"h{t}_{s}", tag=f"bank{HALVES * t + s}")
 
+        for w in range(2):
+            nc.tensor.matmul_mx(
+                out=h[PACK - 1, HALVES - 1][:],
+                lhsT=x_codes[0][:, 0:P].bitcast(FP8X4),
+                lhsT_scale=x_plane[:, 0:P],
+                rhs=x_codes[0][:].bitcast(FP8X4),
+                rhs_scale=x_plane[:, 0:BANK],
+                start=True,
+                stop=True,
+            )
+
         w1_bf = keep.tile([P, PACK, P, PACK], BF16, name="w1_bf", align_bytes=64)
 
         def deal_w1(copy, c, t0, t1):
@@ -107,15 +118,16 @@ def tile_picked_inorm_none_p_kernel(tc, x_words, x_scales, w1, w2, gamma, offs, 
         affine = {}
 
         def product(t, s):
-            nc.tensor.matmul_mx(
-                out=h[t, s][:],
-                lhsT=w1_codes[t][:].bitcast(FP8X4),
-                lhsT_scale=w1_plane[t][:],
-                rhs=x_codes[s][:].bitcast(FP8X4),
-                rhs_scale=x_plane[:, s * BANK : (s + 1) * BANK],
-                start=True,
-                stop=True,
-            )
+            for c0 in range(0, BANK, RUN):
+                nc.tensor.matmul_mx(
+                    out=h[t, s][:, c0 : c0 + RUN],
+                    lhsT=w1_codes[t][:].bitcast(FP8X4),
+                    lhsT_scale=w1_plane[t][:],
+                    rhs=x_codes[s][:, c0 : c0 + RUN].bitcast(FP8X4),
+                    rhs_scale=x_plane[:, s * BANK + c0 : s * BANK + c0 + RUN],
+                    start=True,
+                    stop=True,
+                )
 
         def stats_on_vector(t, s):
             nc.vector.bn_stats(stats[t][:, s].rearrange("p r e -> p (r e)"), h[t, s][:])

@@ -39,7 +39,6 @@ def tile_picked_inorm_none_p_kernel(tc, x_words, x_scales, w1, w2, gamma, offs, 
         table_words = keep.tile([P, T], U32, name="table_words", align_bytes=64)
         table_scales = keep.tile([P, T], U8, name="table_scales", tag="scales_then_weights", align_bytes=64)
         w1_first = keep.tile([P, 2, H], F32, name="w1_first")
-        gain = keep.tile([P, PACK], F32, name="gain")
         x_codes = [keep.tile([P, BANK], U32, name=f"x_codes{s}", align_bytes=64) for s in range(HALVES)]
         picked_scales = keep.tile([P, S], U8, name="picked_scales", align_bytes=64)
         x_plane = keep.tile([P, S], U8, name="x_plane", align_bytes=64)
@@ -52,17 +51,12 @@ def tile_picked_inorm_none_p_kernel(tc, x_words, x_scales, w1, w2, gamma, offs, 
         nc.sync.dma_start(table_words[:].bitcast(I32), x_words[0].rearrange("p n t -> p (n t)").bitcast(I32))
         w1_rows = w1.rearrange("(p j) c -> p j c", j=PACK)
         nc.sync.dma_start(w1_first[:], w1_rows[:, 0:2, :])
-        nc.gpsimd.dma_start(gain[:], gamma.rearrange("(p t) o -> p (t o)", t=PACK))
 
         warm = keep.tile([P, 1], F32, name="warm")
         warm_out = keep.tile([P, 1], F32, name="warm_out")
-        nc.gpsimd.memset(warm[:], 1.0)
+        nc.vector.memset(warm[:], 1.0)
         nc.scalar.activation(warm_out[:], warm[:], ACT.Abs_reciprocal_sqrt)
 
-        factors = keep.tile([P, PACK, 2], F32, name="factors")
-        minus_gain = keep.tile([P, PACK], F32, name="minus_gain")
-        nc.gpsimd.tensor_copy(factors[:, :, 0], gain[:])
-        nc.gpsimd.tensor_scalar(minus_gain[:], gain[:], -1.0, 0.0, ALU.mult, ALU.add)
         stats = [keep.tile([P, HALVES, 2, 3], F32, name=f"stats{t}") for t in range(PACK)]
         nc.vector.memset(stats[1][:, 0, :, 0], float(RUN))
 
@@ -72,11 +66,13 @@ def tile_picked_inorm_none_p_kernel(tc, x_words, x_scales, w1, w2, gamma, offs, 
                 x_plane[QUADRANT * q : QUADRANT * q + 4, :].bitcast(I32),
                 picked_scales[SCALE_ROW0 + 4 * q : SCALE_ROW0 + 4 * q + 4, :].bitcast(I32),
             )
-        late_weights = keep.tile([P, 2 * H + PACK * N], F32, name="late_weights", tag="scales_then_weights", align_bytes=64)
+        late_weights = keep.tile([P, 2 * H + PACK * N + PACK], F32, name="late_weights", tag="scales_then_weights", align_bytes=64)
         w1_raw = [w1_first[:], late_weights[:, 0 : 2 * H].rearrange("p (e c) -> p e c", e=2)]
-        w2_raw = late_weights[:, 2 * H :].rearrange("p (t n) -> p t n", t=PACK)
+        w2_raw = late_weights[:, 2 * H : 2 * H + PACK * N].rearrange("p (t n) -> p t n", t=PACK)
+        gain = late_weights[:, 2 * H + PACK * N :]
         nc.sync.dma_start(w1_raw[1], w1_rows[:, 2:4, :])
         nc.sync.dma_start(w2_raw, w2.rearrange("(p t) n -> p t n", t=PACK))
+        nc.sync.dma_start(gain, gamma.rearrange("(p t) o -> p (t o)", t=PACK))
         for s in range(HALVES):
             nc.vector.tensor_copy(x_codes[s][:], table_words[:].indirect(offsets[:, s * BANK // GROUP : (s + 1) * BANK // GROUP]))
 
@@ -113,6 +109,11 @@ def tile_picked_inorm_none_p_kernel(tc, x_words, x_scales, w1, w2, gamma, offs, 
         w1_plane = [keep.tile([P, P], U8, name=f"w1_plane{t}", align_bytes=64) for t in range(PACK)]
         for t in range(PACK):
             nc.vector.quantize_mx(out=w1_codes[t][:].bitcast(FP8X4), scales=w1_plane[t][:], in_=w1_bf[:, t].rearrange("p m j -> p (m j)"))
+
+        factors = keep.tile([P, PACK, 2], F32, name="factors")
+        minus_gain = keep.tile([P, PACK], F32, name="minus_gain")
+        nc.scalar.copy(factors[:, :, 0], gain)
+        nc.scalar.activation(minus_gain[:], gain, ACT.Identity, scale=-1.0)
 
         z_rows = [keep.tile([P, PACK, BANK], BF16, name=f"z_rows{s}", align_bytes=64) for s in range(HALVES)]
         affine = {}

@@ -26,7 +26,7 @@ SCALE_ROW0 = P - K // 32
 RUN = BANK // 2
 NEIGHBOURS = 4
 CHUNKS = ((0, 256), (256, 256), (512, 256), (768, 128), (896, 128))
-SCALAR_TAIL = 64
+SCALAR_TAIL = 96
 
 
 def tile_picked_inorm_none_p_kernel(tc, x_words, x_scales, w1, w2, gamma, offs, out):
@@ -59,6 +59,9 @@ def tile_picked_inorm_none_p_kernel(tc, x_words, x_scales, w1, w2, gamma, offs, 
 
         stats = [keep.tile([P, HALVES, 2, 3], F32, name=f"stats{t}") for t in range(PACK)]
         nc.vector.memset(stats[1][:, 0, :, 0], float(RUN))
+
+        moments = [keep.tile([P, 3], F32, name=f"moments{t}") for t in range(PACK)]
+        nc.vector.memset(moments[PACK - 1][:, 0:1], -1.0)
 
         nc.vector.tensor_copy(picked_scales[:], table_scales[:].indirect(offsets[:]))
         for q in range(P // QUADRANT):
@@ -110,9 +113,10 @@ def tile_picked_inorm_none_p_kernel(tc, x_words, x_scales, w1, w2, gamma, offs, 
         for t in range(PACK):
             nc.vector.quantize_mx(out=w1_codes[t][:].bitcast(FP8X4), scales=w1_plane[t][:], in_=w1_bf[:, t].rearrange("p m j -> p (m j)"))
 
-        factors = keep.tile([P, PACK, 2], F32, name="factors")
+        factors = keep.tile([P, PACK, 3], F32, name="factors")
         minus_gain = keep.tile([P, PACK], F32, name="minus_gain")
-        nc.scalar.copy(factors[:, :, 0], gain)
+        nc.scalar.activation(factors[:, 1, 0:1], gain[:, 1:2], ACT.Identity, scale=float(RUN))
+        nc.scalar.copy(factors[:, :, 1], gain)
         nc.scalar.activation(minus_gain[:], gain, ACT.Identity, scale=-1.0)
 
         z_rows = [keep.tile([P, PACK, BANK], BF16, name=f"z_rows{s}", align_bytes=64) for s in range(HALVES)]
@@ -133,29 +137,34 @@ def tile_picked_inorm_none_p_kernel(tc, x_words, x_scales, w1, w2, gamma, offs, 
         def stats_on_vector(t, s):
             nc.vector.bn_stats(stats[t][:, s].rearrange("p r e -> p (r e)"), h[t, s][:])
 
+        scaled_h = keep.tile([P, BANK], F32, name="scaled_h")
+
         def stats_on_scalar(t, s):
             spent = keep.tile([P, BANK], BF16, name="spent")
             for r in range(2):
                 cols = slice(r * RUN, (r + 1) * RUN)
-                nc.scalar.activation(spent[:, cols], h[t, s][:, cols], ACT.Identity, scale=1.0 / RUN, accum_out=stats[t][:, s, r, 1:2])
+                nc.scalar.activation(scaled_h[:, cols], h[t, s][:, cols], ACT.Identity, scale=1.0 / RUN, accum_out=stats[t][:, s, r, 1:2])
             for r in range(2):
                 cols = slice(r * RUN, (r + 1) * RUN)
                 nc.scalar.activation(spent[:, cols], h[t, s][:, cols], ACT.Square, scale=-1.0, bias=stats[t][:, s, r, 1:2], accum_out=stats[t][:, s, r, 2:3])
 
         def affine_of(t):
-            moments = keep.tile([P, 2], F32, name=f"moments{t}")
-            nc.vector.bn_aggr(moments[:], stats[t][:].rearrange("p s r e -> p (s r e)"))
+            nc.vector.bn_aggr(moments[t][:, 1:3], stats[t][:].rearrange("p s r e -> p (s r e)"))
             rstd = keep.tile([P, 1], F32, name=f"rstd{t}")
-            nc.scalar.activation(rstd[:], moments[:, 1:2], ACT.Abs_reciprocal_sqrt, bias=EPS)
-            nc.scalar.activation(factors[:, t, 1:2], moments[:, 0:1], ACT.Identity, scale=minus_gain[:, t : t + 1])
-            affine[t] = keep.tile([P, 2], F32, name=f"affine{t}")
-            nc.scalar.activation(affine[t][:], factors[:, t, :], ACT.Identity, scale=rstd[:])
+            nc.scalar.activation(rstd[:], moments[t][:, 2:3], ACT.Abs_reciprocal_sqrt, bias=EPS)
+            affine[t] = keep.tile([P, 3], F32, name=f"affine{t}")
+            first = 0 if t == 1 else 1
+            if t == PACK - 1:
+                nc.vector.tensor_scalar(affine[t][:, 1:3], moments[t][:, 0:2], rstd[:], minus_gain[:, t : t + 1], ALU.mult, ALU.mult)
+            else:
+                nc.scalar.activation(factors[:, t, 2:3], moments[t][:, 1:2], ACT.Identity, scale=minus_gain[:, t : t + 1])
+                nc.scalar.activation(affine[t][:, first:], factors[:, t, first:], ACT.Identity, scale=rstd[:])
 
         def normalise_on_scalar(t, s):
-            nc.scalar.activation(z_rows[s][:, t, :], h[t, s][:], ACT.Identity, bias=affine[t][:, 1:2], scale=affine[t][:, 0:1])
+            nc.scalar.activation(z_rows[s][:, t, :], h[t, s][:], ACT.Identity, bias=affine[t][:, 2:3], scale=affine[t][:, 1:2])
 
         def normalise_on_vector(t, s, c0, c1):
-            nc.vector.tensor_scalar(z_rows[s][:, t, c0:c1], h[t, s][:, c0:c1], affine[t][:, 0:1], affine[t][:, 1:2], ALU.mult, ALU.add)
+            nc.vector.tensor_scalar(z_rows[s][:, t, c0:c1], h[t, s][:, c0:c1], affine[t][:, 1:2], affine[t][:, 2:3], ALU.mult, ALU.add)
 
         for pair in ((0, 1), (2,), (3,)):
             for s in range(HALVES):
@@ -174,10 +183,11 @@ def tile_picked_inorm_none_p_kernel(tc, x_words, x_scales, w1, w2, gamma, offs, 
         nc.scalar.copy(w2_bf[:].rearrange("p (c i) t -> p c t i", i=NEIGHBOURS), w2_raw.rearrange("p t (c i) -> p c t i", i=NEIGHBOURS))
         nc.vector.quantize_mx(out=w2_codes[:].bitcast(FP8X4), scales=w2_plane[:], in_=w2_bf[:].rearrange("p n t -> p (n t)"))
 
-        for t in (0, 1):
-            for s in range(HALVES):
-                normalise_on_scalar(t, s)
-        normalise_on_vector(2, 0, 0, BANK)
+        nc.gpsimd.tensor_scalar(z_rows[0][:, 1, :], scaled_h[:], affine[1][:, 0:1], affine[1][:, 2:3], ALU.mult, ALU.add)
+        for t, s in ((0, 0), (0, 1), (1, 1)):
+            normalise_on_scalar(t, s)
+        for first, width in CHUNKS[:2]:
+            normalise_on_vector(2, 0, first, first + width)
         normalise_on_scalar(2, 1)
         for first, width in CHUNKS[:2]:
             normalise_on_vector(3, 0, first, first + width)
@@ -192,13 +202,8 @@ def tile_picked_inorm_none_p_kernel(tc, x_words, x_scales, w1, w2, gamma, offs, 
                 z_rows[s][:, :, c0 + n0 : c0 + n1].rearrange("p t (c i) -> p c t i", i=NEIGHBOURS),
             )
 
-        last = len(CHUNKS) - 1
-        for c, (first, width) in enumerate(CHUNKS[:last]):
-            weave(nc.vector.tensor_copy if first < BANK else nc.scalar.copy, c, 0, width)
-        weave(nc.scalar.copy, last, 0, SCALAR_TAIL)
-        weave(nc.vector.tensor_copy, last, SCALAR_TAIL, CHUNKS[last][1])
-
-        for c, (first, width) in enumerate(CHUNKS):
+        def second_layer(c):
+            first, width = CHUNKS[c]
             z_codes = keep.tile([P, width], U32, name=f"z_codes{c}", align_bytes=64)
             z_plane = keep.tile([P, width], U8, name=f"z_plane{c}", align_bytes=64)
             nc.vector.quantize_mx(out=z_codes[:].bitcast(FP8X4), scales=z_plane[:], in_=z_bf[c][:].rearrange("p n t -> p (n t)"))
@@ -216,3 +221,15 @@ def tile_picked_inorm_none_p_kernel(tc, x_words, x_scales, w1, w2, gamma, offs, 
             drain = nc.vector.tensor_copy if c == last else nc.scalar.copy
             drain(result[:], y[:])
             nc.sync.dma_start(out[:, first : first + width], result[:])
+
+        last = len(CHUNKS) - 1
+        for c in (2, 3):
+            weave(nc.scalar.copy, c, 0, CHUNKS[c][1])
+        weave(nc.scalar.copy, last, 0, SCALAR_TAIL)
+        for c in (0, 1):
+            weave(nc.vector.tensor_copy, c, 0, CHUNKS[c][1])
+        for c in (0, 1):
+            second_layer(c)
+        weave(nc.vector.tensor_copy, last, SCALAR_TAIL, CHUNKS[last][1])
+        for c in range(2, len(CHUNKS)):
+            second_layer(c)

@@ -26,7 +26,7 @@ SCALE_ROW0 = P - K // 32
 RUN = BANK // 2
 NEIGHBOURS = 4
 CHUNKS = ((0, 256), (256, 256), (512, 256), (768, 128), (896, 128))
-SCALAR_TAIL = 96
+SCALAR_TAIL = 32
 
 
 def tile_picked_inorm_none_p_kernel(tc, x_words, x_scales, w1, w2, gamma, offs, out):
@@ -57,11 +57,11 @@ def tile_picked_inorm_none_p_kernel(tc, x_words, x_scales, w1, w2, gamma, offs, 
         nc.vector.memset(warm[:], 1.0)
         nc.scalar.activation(warm_out[:], warm[:], ACT.Abs_reciprocal_sqrt)
 
-        stats = [keep.tile([P, HALVES, 2, 3], F32, name=f"stats{t}") for t in range(PACK)]
-        nc.vector.memset(stats[1][:, 0, :, 0], float(RUN))
+        stats = {t: keep.tile([P, HALVES, 2, 3], F32, name=f"stats{t}") for t in (0, 2, 3)}
 
         moments = [keep.tile([P, 3], F32, name=f"moments{t}") for t in range(PACK)]
-        nc.vector.memset(moments[PACK - 1][:, 0:1], -1.0)
+        for t in range(PACK):
+            nc.vector.memset(moments[t][:, 0:1], -float(S) if t == 1 else -1.0)
 
         nc.vector.tensor_copy(picked_scales[:], table_scales[:].indirect(offsets[:]))
         for q in range(P // QUADRANT):
@@ -95,7 +95,7 @@ def tile_picked_inorm_none_p_kernel(tc, x_words, x_scales, w1, w2, gamma, offs, 
                 stop=True,
             )
 
-        w1_bf = keep.tile([P, PACK, P, PACK], BF16, name="w1_bf", align_bytes=64)
+        w1_bf = keep.tile([P, PACK, P, PACK], BF16, name="w1_bf", tag="dealt_weights", align_bytes=64)
 
         def deal_w1(copy, c, t0, t1):
             src = w1_raw[c].rearrange("p e (m t) -> p m e t", t=PACK)[:, :, :, t0:t1]
@@ -113,10 +113,8 @@ def tile_picked_inorm_none_p_kernel(tc, x_words, x_scales, w1, w2, gamma, offs, 
         for t in range(PACK):
             nc.vector.quantize_mx(out=w1_codes[t][:].bitcast(FP8X4), scales=w1_plane[t][:], in_=w1_bf[:, t].rearrange("p m j -> p (m j)"))
 
-        factors = keep.tile([P, PACK, 3], F32, name="factors")
+        factors = keep.tile([P, PACK, 2], F32, name="factors")
         minus_gain = keep.tile([P, PACK], F32, name="minus_gain")
-        nc.scalar.activation(factors[:, 1, 0:1], gain[:, 1:2], ACT.Identity, scale=float(RUN))
-        nc.scalar.copy(factors[:, :, 1], gain)
         nc.scalar.activation(minus_gain[:], gain, ACT.Identity, scale=-1.0)
 
         z_rows = [keep.tile([P, PACK, BANK], BF16, name=f"z_rows{s}", align_bytes=64) for s in range(HALVES)]
@@ -137,55 +135,60 @@ def tile_picked_inorm_none_p_kernel(tc, x_words, x_scales, w1, w2, gamma, offs, 
         def stats_on_vector(t, s):
             nc.vector.bn_stats(stats[t][:, s].rearrange("p r e -> p (r e)"), h[t, s][:])
 
-        scaled_h = keep.tile([P, BANK], F32, name="scaled_h")
+        scaled_h = keep.tile([P, S], F32, name="scaled_h")
 
-        def stats_on_scalar(t, s):
-            spent = keep.tile([P, BANK], BF16, name="spent")
-            for r in range(2):
-                cols = slice(r * RUN, (r + 1) * RUN)
-                nc.scalar.activation(scaled_h[:, cols], h[t, s][:, cols], ACT.Identity, scale=1.0 / RUN, accum_out=stats[t][:, s, r, 1:2])
-            for r in range(2):
-                cols = slice(r * RUN, (r + 1) * RUN)
-                nc.scalar.activation(spent[:, cols], h[t, s][:, cols], ACT.Square, scale=-1.0, bias=stats[t][:, s, r, 1:2], accum_out=stats[t][:, s, r, 2:3])
+        def stats_on_scalar(t):
+            part = keep.tile([P, HALVES], F32, name="part")
+            for s in range(HALVES):
+                nc.scalar.activation(scaled_h[:, s * BANK : (s + 1) * BANK], h[t, s][:], ACT.Identity, scale=1.0 / S, accum_out=part[:, s : s + 1])
+            nc.scalar.activation(moments[t][:, 1:2], part[:, 0:1], ACT.Identity, bias=part[:, 1:2])
+            spent = z_rows[0][:, 0::2, :]
+            nc.scalar.activation(spent, scaled_h[:].rearrange("p (s n) -> p s n", s=HALVES), ACT.Square, scale=-float(S), bias=moments[t][:, 1:2], accum_out=moments[t][:, 2:3])
+            rstd = keep.tile([P, 1], F32, name=f"rstd{t}")
+            nc.scalar.activation(rstd[:], moments[t][:, 2:3], ACT.Abs_reciprocal_sqrt, scale=1.0 / S, bias=EPS)
+            affine[t] = keep.tile([P, 2], F32, name=f"affine{t}")
+            nc.gpsimd.tensor_scalar(affine[t][:], moments[t][:, 0:2], rstd[:], minus_gain[:, t : t + 1], ALU.mult, ALU.mult)
 
         def affine_of(t):
             nc.vector.bn_aggr(moments[t][:, 1:3], stats[t][:].rearrange("p s r e -> p (s r e)"))
             rstd = keep.tile([P, 1], F32, name=f"rstd{t}")
             nc.scalar.activation(rstd[:], moments[t][:, 2:3], ACT.Abs_reciprocal_sqrt, bias=EPS)
-            affine[t] = keep.tile([P, 3], F32, name=f"affine{t}")
-            first = 0 if t == 1 else 1
-            if t == PACK - 1:
-                nc.vector.tensor_scalar(affine[t][:, 1:3], moments[t][:, 0:2], rstd[:], minus_gain[:, t : t + 1], ALU.mult, ALU.mult)
+            affine[t] = keep.tile([P, 2], F32, name=f"affine{t}")
+            if t >= 2:
+                nc.vector.tensor_scalar(affine[t][:], moments[t][:, 0:2], rstd[:], minus_gain[:, t : t + 1], ALU.mult, ALU.mult)
             else:
-                nc.scalar.activation(factors[:, t, 2:3], moments[t][:, 1:2], ACT.Identity, scale=minus_gain[:, t : t + 1])
-                nc.scalar.activation(affine[t][:, first:], factors[:, t, first:], ACT.Identity, scale=rstd[:])
+                nc.scalar.activation(factors[:, t, :], moments[t][:, 0:2], ACT.Identity, scale=minus_gain[:, t : t + 1])
+                nc.scalar.activation(affine[t][:], factors[:, t, :], ACT.Identity, scale=rstd[:])
 
         def normalise_on_scalar(t, s):
-            nc.scalar.activation(z_rows[s][:, t, :], h[t, s][:], ACT.Identity, bias=affine[t][:, 2:3], scale=affine[t][:, 1:2])
+            nc.scalar.activation(z_rows[s][:, t, :], h[t, s][:], ACT.Identity, bias=affine[t][:, 1:2], scale=affine[t][:, 0:1])
 
         def normalise_on_vector(t, s, c0, c1):
-            nc.vector.tensor_scalar(z_rows[s][:, t, c0:c1], h[t, s][:, c0:c1], affine[t][:, 1:2], affine[t][:, 2:3], ALU.mult, ALU.add)
+            nc.vector.tensor_scalar(z_rows[s][:, t, c0:c1], h[t, s][:, c0:c1], affine[t][:, 0:1], affine[t][:, 1:2], ALU.mult, ALU.add)
 
         for pair in ((0, 1), (2,), (3,)):
             for s in range(HALVES):
                 for t in pair:
                     product(t, s)
-        stats_on_scalar(1, 0)
-        for t in range(PACK):
+        w2_bf = keep.tile([P, N, PACK], BF16, name="w2_bf", tag="dealt_weights", align_bytes=64)
+        nc.gpsimd.tensor_scalar(w2_bf[:], w2_raw.rearrange("p t n -> p n t"), 1.0, 0.0, ALU.mult, ALU.add)
+        for s in range(HALVES):
+            stats_on_vector(0, s)
+        affine_of(0)
+        stats_on_scalar(1)
+        for t in (2, 3):
             for s in range(HALVES):
-                if (t, s) != (1, 0):
-                    stats_on_vector(t, s)
+                stats_on_vector(t, s)
             affine_of(t)
 
-        w2_bf = keep.tile([P, N, PACK], BF16, name="w2_bf", align_bytes=64)
         w2_codes = keep.tile([P, N], U32, name="w2_codes", align_bytes=64)
         w2_plane = keep.tile([P, N], U8, name="w2_plane", align_bytes=64)
-        nc.scalar.copy(w2_bf[:].rearrange("p (c i) t -> p c t i", i=NEIGHBOURS), w2_raw.rearrange("p t (c i) -> p c t i", i=NEIGHBOURS))
         nc.vector.quantize_mx(out=w2_codes[:].bitcast(FP8X4), scales=w2_plane[:], in_=w2_bf[:].rearrange("p n t -> p (n t)"))
 
-        nc.gpsimd.tensor_scalar(z_rows[0][:, 1, :], scaled_h[:], affine[1][:, 0:1], affine[1][:, 2:3], ALU.mult, ALU.add)
-        for t, s in ((0, 0), (0, 1), (1, 1)):
-            normalise_on_scalar(t, s)
+        for s in range(HALVES):
+            nc.gpsimd.tensor_scalar(z_rows[s][:, 1, :], scaled_h[:, s * BANK : (s + 1) * BANK], affine[1][:, 0:1], affine[1][:, 1:2], ALU.mult, ALU.add)
+        for s in range(HALVES):
+            normalise_on_scalar(0, s)
         for first, width in CHUNKS[:2]:
             normalise_on_vector(2, 0, first, first + width)
         normalise_on_scalar(2, 1)

@@ -59,9 +59,9 @@ def tile_picked_inorm_none_p_kernel(tc, x_words, x_scales, w1, w2, gamma, offs, 
 
         stats = {t: keep.tile([P, HALVES, 2, 3], F32, name=f"stats{t}") for t in (0, 2, 3)}
 
-        moments = [keep.tile([P, 3], F32, name=f"moments{t}") for t in range(PACK)]
-        for t in range(PACK):
-            nc.vector.memset(moments[t][:, 0:1], -float(S) if t == 1 else -1.0)
+        terms = keep.tile([P, PACK, 2, 6], F32, name="terms")
+        nc.vector.memset(terms[:, :, 0, 0], -1.0)
+        nc.vector.memset(terms[:, 1, 0, 0:1], -float(S))
 
         nc.vector.tensor_copy(picked_scales[:], table_scales[:].indirect(offsets[:]))
         for q in range(P // QUADRANT):
@@ -113,9 +113,7 @@ def tile_picked_inorm_none_p_kernel(tc, x_words, x_scales, w1, w2, gamma, offs, 
         for t in range(PACK):
             nc.vector.quantize_mx(out=w1_codes[t][:].bitcast(FP8X4), scales=w1_plane[t][:], in_=w1_bf[:, t].rearrange("p m j -> p (m j)"))
 
-        factors = keep.tile([P, PACK, 2], F32, name="factors")
-        minus_gain = keep.tile([P, PACK], F32, name="minus_gain")
-        nc.scalar.activation(minus_gain[:], gain, ACT.Identity, scale=-1.0)
+        nc.scalar.activation(terms[:, :, :, 4], gain.unsqueeze(2).to_broadcast([P, PACK, 2]), ACT.Identity, scale=-1.0)
 
         z_rows = [keep.tile([P, PACK, BANK], BF16, name=f"z_rows{s}", align_bytes=64) for s in range(HALVES)]
         affine = {}
@@ -141,24 +139,19 @@ def tile_picked_inorm_none_p_kernel(tc, x_words, x_scales, w1, w2, gamma, offs, 
             part = keep.tile([P, HALVES], F32, name="part")
             for s in range(HALVES):
                 nc.scalar.activation(scaled_h[:, s * BANK : (s + 1) * BANK], h[t, s][:], ACT.Identity, scale=1.0 / S, accum_out=part[:, s : s + 1])
-            nc.scalar.activation(moments[t][:, 1:2], part[:, 0:1], ACT.Identity, bias=part[:, 1:2])
+            nc.scalar.activation(terms[:, t, 1, 0:1], part[:, 0:1], ACT.Identity, bias=part[:, 1:2])
             spent = z_rows[0][:, 0::2, :]
-            nc.scalar.activation(spent, scaled_h[:].rearrange("p (s n) -> p s n", s=HALVES), ACT.Square, scale=-float(S), bias=moments[t][:, 1:2], accum_out=moments[t][:, 2:3])
+            nc.scalar.activation(spent, scaled_h[:].rearrange("p (s n) -> p s n", s=HALVES), ACT.Square, scale=-float(S), bias=terms[:, t, 1, 0:1], accum_out=terms[:, t, 1, 1:2])
             rstd = keep.tile([P, 1], F32, name=f"rstd{t}")
-            nc.scalar.activation(rstd[:], moments[t][:, 2:3], ACT.Abs_reciprocal_sqrt, scale=1.0 / S, bias=EPS)
+            nc.scalar.activation(rstd[:], terms[:, t, 1, 1:2], ACT.Abs_reciprocal_sqrt, scale=1.0 / S, bias=EPS)
             affine[t] = keep.tile([P, 2], F32, name=f"affine{t}")
-            nc.gpsimd.tensor_scalar(affine[t][:], moments[t][:, 0:2], rstd[:], minus_gain[:, t : t + 1], ALU.mult, ALU.mult)
+            nc.gpsimd.tensor_scalar(affine[t][:], terms[:, t, :, 0], rstd[:], terms[:, t, 0, 4:5], ALU.mult, ALU.mult)
 
         def affine_of(t):
-            nc.vector.bn_aggr(moments[t][:, 1:3], stats[t][:].rearrange("p s r e -> p (s r e)"))
-            rstd = keep.tile([P, 1], F32, name=f"rstd{t}")
-            nc.scalar.activation(rstd[:], moments[t][:, 2:3], ACT.Abs_reciprocal_sqrt, bias=EPS)
+            nc.vector.bn_aggr(terms[:, t, 1, 0:2], stats[t][:].rearrange("p s r e -> p (s r e)"))
+            nc.scalar.activation(terms[:, t, :, 2], terms[:, t, 1, 1:2].to_broadcast([P, 2]), ACT.Abs_reciprocal_sqrt, bias=EPS)
             affine[t] = keep.tile([P, 2], F32, name=f"affine{t}")
-            if t >= 2:
-                nc.vector.tensor_scalar(affine[t][:], moments[t][:, 0:2], rstd[:], minus_gain[:, t : t + 1], ALU.mult, ALU.mult)
-            else:
-                nc.scalar.activation(factors[:, t, :], moments[t][:, 0:2], ACT.Identity, scale=minus_gain[:, t : t + 1])
-                nc.scalar.activation(affine[t][:], factors[:, t, :], ACT.Identity, scale=rstd[:])
+            nc.vector.tensor_reduce(affine[t][:], terms[:, t, :, 0:6:2], mybir.AxisListType.X, ALU.mult)
 
         def normalise_on_scalar(t, s):
             nc.scalar.activation(z_rows[s][:, t, :], h[t, s][:], ACT.Identity, bias=affine[t][:, 1:2], scale=affine[t][:, 0:1])
@@ -170,8 +163,8 @@ def tile_picked_inorm_none_p_kernel(tc, x_words, x_scales, w1, w2, gamma, offs, 
             for s in range(HALVES):
                 for t in pair:
                     product(t, s)
-        w2_bf = keep.tile([P, N, PACK], BF16, name="w2_bf", tag="dealt_weights", align_bytes=64)
-        nc.gpsimd.tensor_scalar(w2_bf[:], w2_raw.rearrange("p t n -> p n t"), 1.0, 0.0, ALU.mult, ALU.add)
+        w2_bf = keep.tile([P, N, PACK], BF16, name="w2_bf", align_bytes=64)
+        nc.scalar.copy(w2_bf[:].rearrange("p (c i) t -> p c t i", i=NEIGHBOURS), w2_raw.rearrange("p t (c i) -> p c t i", i=NEIGHBOURS))
         for s in range(HALVES):
             stats_on_vector(0, s)
         affine_of(0)
@@ -187,11 +180,11 @@ def tile_picked_inorm_none_p_kernel(tc, x_words, x_scales, w1, w2, gamma, offs, 
 
         for s in range(HALVES):
             nc.gpsimd.tensor_scalar(z_rows[s][:, 1, :], scaled_h[:, s * BANK : (s + 1) * BANK], affine[1][:, 0:1], affine[1][:, 1:2], ALU.mult, ALU.add)
-        for s in range(HALVES):
-            normalise_on_scalar(0, s)
+        normalise_on_scalar(0, 0)
         for first, width in CHUNKS[:2]:
-            normalise_on_vector(2, 0, first, first + width)
-        normalise_on_scalar(2, 1)
+            normalise_on_vector(0, 1, first, first + width)
+        for s in range(HALVES):
+            normalise_on_scalar(2, s)
         for first, width in CHUNKS[:2]:
             normalise_on_vector(3, 0, first, first + width)
         normalise_on_scalar(3, 1)

@@ -26,7 +26,7 @@ SCALE_ROW0 = P - K // 32
 RUN = BANK // 2
 NEIGHBOURS = 4
 CHUNKS = ((0, 256), (256, 256), (512, 256), (768, 128), (896, 128))
-SCALAR_TAIL = 32
+SCALAR_TAIL = 64
 
 
 def tile_picked_inorm_none_p_kernel(tc, x_words, x_scales, w1, w2, gamma, offs, out):
@@ -38,7 +38,7 @@ def tile_picked_inorm_none_p_kernel(tc, x_words, x_scales, w1, w2, gamma, offs, 
         offsets = keep.tile([P, S // GROUP], U16, name="offsets")
         table_words = keep.tile([P, T], U32, name="table_words", align_bytes=64)
         table_scales = keep.tile([P, T], U8, name="table_scales", tag="scales_then_weights", align_bytes=64)
-        w1_first = keep.tile([P, 2, H], F32, name="w1_first")
+        w1_first = keep.tile([P, 2, H // 2], F32, name="w1_first")
         x_codes = [keep.tile([P, BANK], U32, name=f"x_codes{s}", align_bytes=64) for s in range(HALVES)]
         picked_scales = keep.tile([P, S], U8, name="picked_scales", align_bytes=64)
         x_plane = keep.tile([P, S], U8, name="x_plane", align_bytes=64)
@@ -50,7 +50,7 @@ def tile_picked_inorm_none_p_kernel(tc, x_words, x_scales, w1, w2, gamma, offs, 
         nc.sync.dma_start(offsets[:], offs)
         nc.sync.dma_start(table_words[:].bitcast(I32), x_words[0].rearrange("p n t -> p (n t)").bitcast(I32))
         w1_rows = w1.rearrange("(p j) c -> p j c", j=PACK)
-        nc.sync.dma_start(w1_first[:], w1_rows[:, 0:2, :])
+        nc.sync.dma_start(w1_first[:], w1_rows[:, 0:2, 0 : H // 2])
 
         warm = keep.tile([P, 1], F32, name="warm")
         warm_out = keep.tile([P, 1], F32, name="warm_out")
@@ -69,11 +69,13 @@ def tile_picked_inorm_none_p_kernel(tc, x_words, x_scales, w1, w2, gamma, offs, 
                 x_plane[QUADRANT * q : QUADRANT * q + 4, :].bitcast(I32),
                 picked_scales[SCALE_ROW0 + 4 * q : SCALE_ROW0 + 4 * q + 4, :].bitcast(I32),
             )
-        late_weights = keep.tile([P, 2 * H + PACK * N + PACK], F32, name="late_weights", tag="scales_then_weights", align_bytes=64)
-        w1_raw = [w1_first[:], late_weights[:, 0 : 2 * H].rearrange("p (e c) -> p e c", e=2)]
-        w2_raw = late_weights[:, 2 * H : 2 * H + PACK * N].rearrange("p (t n) -> p t n", t=PACK)
-        gain = late_weights[:, 2 * H + PACK * N :]
-        nc.sync.dma_start(w1_raw[1], w1_rows[:, 2:4, :])
+        late_weights = keep.tile([P, 3 * H + PACK * N + PACK], F32, name="late_weights", tag="scales_then_weights", align_bytes=64)
+        w1_second = late_weights[:, 0:H].rearrange("p (e c) -> p e c", e=2)
+        w1_third = late_weights[:, H : 3 * H].rearrange("p (e c) -> p e c", e=2)
+        w2_raw = late_weights[:, 3 * H : 3 * H + PACK * N].rearrange("p (t n) -> p t n", t=PACK)
+        gain = late_weights[:, 3 * H + PACK * N :]
+        nc.sync.dma_start(w1_second, w1_rows[:, 0:2, H // 2 : H])
+        nc.sync.dma_start(w1_third, w1_rows[:, 2:4, :])
         nc.sync.dma_start(w2_raw, w2.rearrange("(p t) n -> p t n", t=PACK))
         nc.sync.dma_start(gain, gamma.rearrange("(p t) o -> p (t o)", t=PACK))
         for s in range(HALVES):
@@ -97,16 +99,16 @@ def tile_picked_inorm_none_p_kernel(tc, x_words, x_scales, w1, w2, gamma, offs, 
 
         w1_bf = keep.tile([P, PACK, P, PACK], BF16, name="w1_bf", tag="dealt_weights", align_bytes=64)
 
-        def deal_w1(copy, c, t0, t1):
-            src = w1_raw[c].rearrange("p e (m t) -> p m e t", t=PACK)[:, :, :, t0:t1]
-            dst = w1_bf[:].rearrange("p t m j -> p m j t")[:, :, 2 * c : 2 * c + 2, t0:t1]
+        def deal_w1(copy, raw, j0, m0, m1, t0, t1):
+            src = raw.rearrange("p e (m t) -> p m e t", t=PACK)[:, :, :, t0:t1]
+            dst = w1_bf[:].rearrange("p t m j -> p m j t")[:, m0:m1, j0 : j0 + 2, t0:t1]
             copy(dst, src)
 
-        deal_w1(nc.scalar.copy, 0, 0, 2)
-        deal_w1(nc.scalar.copy, 0, 2, 4)
-        deal_w1(nc.vector.tensor_copy, 1, 0, 1)
-        deal_w1(nc.vector.tensor_copy, 1, 1, 2)
-        deal_w1(nc.scalar.copy, 1, 2, 4)
+        deal_w1(nc.scalar.copy, w1_first[:], 0, 0, P // 2, 0, PACK)
+        deal_w1(nc.scalar.copy, w1_second, 0, P // 2, P, 0, PACK)
+        deal_w1(nc.vector.tensor_copy, w1_third, 2, 0, P, 0, 1)
+        deal_w1(nc.vector.tensor_copy, w1_third, 2, 0, P, 1, 2)
+        deal_w1(nc.scalar.copy, w1_third, 2, 0, P, 2, 4)
 
         w1_codes = [keep.tile([P, P], U32, name=f"w1_codes{t}", align_bytes=64) for t in range(PACK)]
         w1_plane = [keep.tile([P, P], U8, name=f"w1_plane{t}", align_bytes=64) for t in range(PACK)]
@@ -115,7 +117,8 @@ def tile_picked_inorm_none_p_kernel(tc, x_words, x_scales, w1, w2, gamma, offs, 
 
         nc.scalar.activation(terms[:, :, :, 4], gain.unsqueeze(2).to_broadcast([P, PACK, 2]), ACT.Identity, scale=-1.0)
 
-        z_rows = [keep.tile([P, PACK, BANK], BF16, name=f"z_rows{s}", align_bytes=64) for s in range(HALVES)]
+        z_all = keep.tile([P, HALVES, PACK, BANK], BF16, name="z_all", align_bytes=64)
+        z_rows = [z_all[:, s] for s in range(HALVES)]
         affine = {}
 
         def product(t, s):
@@ -140,10 +143,11 @@ def tile_picked_inorm_none_p_kernel(tc, x_words, x_scales, w1, w2, gamma, offs, 
             for s in range(HALVES):
                 nc.scalar.activation(scaled_h[:, s * BANK : (s + 1) * BANK], h[t, s][:], ACT.Identity, scale=1.0 / S, accum_out=part[:, s : s + 1])
             nc.scalar.activation(terms[:, t, 1, 0:1], part[:, 0:1], ACT.Identity, bias=part[:, 1:2])
-            spent = z_rows[0][:, 0::2, :]
-            nc.scalar.activation(spent, scaled_h[:].rearrange("p (s n) -> p s n", s=HALVES), ACT.Square, scale=-float(S), bias=terms[:, t, 1, 0:1], accum_out=terms[:, t, 1, 1:2])
+            spent = z_all[:, :, 0, :]
+            squares = terms[:, t, 1, 1:2]
+            nc.scalar.activation(spent, scaled_h[:].rearrange("p (s n) -> p s n", s=HALVES), ACT.Square, scale=-float(S), bias=terms[:, t, 1, 0:1], accum_out=squares)
             rstd = keep.tile([P, 1], F32, name=f"rstd{t}")
-            nc.scalar.activation(rstd[:], terms[:, t, 1, 1:2], ACT.Abs_reciprocal_sqrt, scale=1.0 / S, bias=EPS)
+            nc.scalar.activation(rstd[:], squares, ACT.Abs_reciprocal_sqrt, scale=1.0 / S, bias=EPS)
             affine[t] = keep.tile([P, 2], F32, name=f"affine{t}")
             nc.gpsimd.tensor_scalar(affine[t][:], terms[:, t, :, 0], rstd[:], terms[:, t, 0, 4:5], ALU.mult, ALU.mult)
 
@@ -178,13 +182,12 @@ def tile_picked_inorm_none_p_kernel(tc, x_words, x_scales, w1, w2, gamma, offs, 
         w2_plane = keep.tile([P, N], U8, name="w2_plane", align_bytes=64)
         nc.vector.quantize_mx(out=w2_codes[:].bitcast(FP8X4), scales=w2_plane[:], in_=w2_bf[:].rearrange("p n t -> p (n t)"))
 
+        nc.gpsimd.tensor_scalar(z_all[:, :, 1, :], scaled_h[:].rearrange("p (s n) -> p s n", s=HALVES), affine[1][:, 0:1], affine[1][:, 1:2], ALU.mult, ALU.add)
         for s in range(HALVES):
-            nc.gpsimd.tensor_scalar(z_rows[s][:, 1, :], scaled_h[:, s * BANK : (s + 1) * BANK], affine[1][:, 0:1], affine[1][:, 1:2], ALU.mult, ALU.add)
-        normalise_on_scalar(0, 0)
+            normalise_on_scalar(0, s)
         for first, width in CHUNKS[:2]:
-            normalise_on_vector(0, 1, first, first + width)
-        for s in range(HALVES):
-            normalise_on_scalar(2, s)
+            normalise_on_vector(2, 0, first, first + width)
+        normalise_on_scalar(2, 1)
         for first, width in CHUNKS[:2]:
             normalise_on_vector(3, 0, first, first + width)
         normalise_on_scalar(3, 1)
@@ -197,6 +200,10 @@ def tile_picked_inorm_none_p_kernel(tc, x_words, x_scales, w1, w2, gamma, offs, 
                 z_bf[c][:, n0:n1, :].rearrange("p (c i) t -> p c t i", i=NEIGHBOURS),
                 z_rows[s][:, :, c0 + n0 : c0 + n1].rearrange("p t (c i) -> p c t i", i=NEIGHBOURS),
             )
+
+        result = [keep.tile([P, RUN], F32, name=f"result{piece}") for piece in range(S // RUN)]
+
+        products = {}
 
         def second_layer(c):
             first, width = CHUNKS[c]
@@ -213,19 +220,25 @@ def tile_picked_inorm_none_p_kernel(tc, x_words, x_scales, w1, w2, gamma, offs, 
                 start=True,
                 stop=True,
             )
-            result = keep.tile([P, width], F32, name=f"result{c}")
-            drain = nc.vector.tensor_copy if c == last else nc.scalar.copy
-            drain(result[:], y[:])
-            nc.sync.dma_start(out[:, first : first + width], result[:])
+            products[c] = y
+
+        def store(copy, c):
+            first, width = CHUNKS[c]
+            piece, c0 = divmod(first, RUN)
+            copy(result[piece][:, c0 : c0 + width], products[c][:])
+            if c0 + width == RUN:
+                nc.sync.dma_start(out[:, piece * RUN : (piece + 1) * RUN], result[piece][:])
 
         last = len(CHUNKS) - 1
-        for c in (2, 3):
+        for c in (1, 3):
             weave(nc.scalar.copy, c, 0, CHUNKS[c][1])
         weave(nc.scalar.copy, last, 0, SCALAR_TAIL)
-        for c in (0, 1):
+        for c in (0, 2):
             weave(nc.vector.tensor_copy, c, 0, CHUNKS[c][1])
-        for c in (0, 1):
+        for c in (0, 1, 2):
             second_layer(c)
         weave(nc.vector.tensor_copy, last, SCALAR_TAIL, CHUNKS[last][1])
-        for c in range(2, len(CHUNKS)):
+        for c in range(3, len(CHUNKS)):
             second_layer(c)
+        for c in range(len(CHUNKS)):
+            store(nc.vector.tensor_copy if c in (2, last) else nc.scalar.copy, c)

@@ -65,7 +65,8 @@ def tile_picked_inorm_none_p_kernel(tc, x_words, x_scales, w1, w2, gamma, offs, 
 
         nc.vector.tensor_copy(picked_scales[:], table_scales[:].indirect(offsets[:]))
         for q in range(P // QUADRANT):
-            nc.sync.dma_start(
+            queue = nc.sync if q % 2 == 0 else nc.scalar
+            queue.dma_start(
                 x_plane[QUADRANT * q : QUADRANT * q + 4, :].bitcast(I32),
                 picked_scales[SCALE_ROW0 + 4 * q : SCALE_ROW0 + 4 * q + 4, :].bitcast(I32),
             )

@@ -26,7 +26,7 @@ SCALE_ROW0 = P - K // 32
 RUN = BANK // 2
 NEIGHBOURS = 4
 CHUNKS = ((0, 256), (256, 256), (512, 256), (768, 128), (896, 128))
-SCALAR_TAIL = 64
+SCALAR_TAIL = 48
 
 
 def tile_picked_inorm_none_p_kernel(tc, x_words, x_scales, w1, w2, gamma, offs, out):
@@ -61,7 +61,6 @@ def tile_picked_inorm_none_p_kernel(tc, x_words, x_scales, w1, w2, gamma, offs, 
 
         terms = keep.tile([P, PACK, 2, 6], F32, name="terms")
         nc.vector.memset(terms[:, :, 0, 0], -1.0)
-        nc.vector.memset(terms[:, 1, 0, 0:1], -float(S))
 
         nc.vector.tensor_copy(picked_scales[:], table_scales[:].indirect(offsets[:]))
         for q in range(P // QUADRANT):
@@ -144,13 +143,14 @@ def tile_picked_inorm_none_p_kernel(tc, x_words, x_scales, w1, w2, gamma, offs, 
             for s in range(HALVES):
                 nc.scalar.activation(scaled_h[:, s * BANK : (s + 1) * BANK], h[t, s][:], ACT.Identity, scale=1.0 / S, accum_out=part[:, s : s + 1])
             nc.scalar.activation(terms[:, t, 1, 0:1], part[:, 0:1], ACT.Identity, bias=part[:, 1:2])
+            centred = keep.tile([P, S], F32, name="centred", tag="centred_then_codes", align_bytes=64)
+            nc.gpsimd.tensor_scalar(centred[:], scaled_h[:], -float(S), terms[:, t, 1, 0:1], ALU.mult, ALU.add)
             spent = z_all[:, :, 0, :]
             squares = terms[:, t, 1, 1:2]
             nc.scalar.activation(spent, scaled_h[:].rearrange("p (s n) -> p s n", s=HALVES), ACT.Square, scale=-float(S), bias=terms[:, t, 1, 0:1], accum_out=squares)
             rstd = keep.tile([P, 1], F32, name=f"rstd{t}")
             nc.scalar.activation(rstd[:], squares, ACT.Abs_reciprocal_sqrt, scale=1.0 / S, bias=EPS)
-            affine[t] = keep.tile([P, 2], F32, name=f"affine{t}")
-            nc.gpsimd.tensor_scalar(affine[t][:], terms[:, t, :, 0], rstd[:], terms[:, t, 0, 4:5], ALU.mult, ALU.mult)
+            nc.gpsimd.tensor_scalar(z_all[:, :, t, :], centred[:].rearrange("p (s n) -> p s n", s=HALVES), rstd[:], terms[:, t, 0, 4:5], ALU.mult, ALU.mult)
 
         def affine_of(t):
             nc.vector.bn_aggr(terms[:, t, 1, 0:2], stats[t][:].rearrange("p s r e -> p (s r e)"))
@@ -179,11 +179,7 @@ def tile_picked_inorm_none_p_kernel(tc, x_words, x_scales, w1, w2, gamma, offs, 
                 stats_on_vector(t, s)
             affine_of(t)
 
-        w2_codes = keep.tile([P, N], U32, name="w2_codes", align_bytes=64)
-        w2_plane = keep.tile([P, N], U8, name="w2_plane", align_bytes=64)
-        nc.vector.quantize_mx(out=w2_codes[:].bitcast(FP8X4), scales=w2_plane[:], in_=w2_bf[:].rearrange("p n t -> p (n t)"))
 
-        nc.gpsimd.tensor_scalar(z_all[:, :, 1, :], scaled_h[:].rearrange("p (s n) -> p s n", s=HALVES), affine[1][:, 0:1], affine[1][:, 1:2], ALU.mult, ALU.add)
         for s in range(HALVES):
             normalise_on_scalar(0, s)
         for first, width in CHUNKS[:2]:
@@ -192,6 +188,10 @@ def tile_picked_inorm_none_p_kernel(tc, x_words, x_scales, w1, w2, gamma, offs, 
         for first, width in CHUNKS[:2]:
             normalise_on_vector(3, 0, first, first + width)
         normalise_on_scalar(3, 1)
+
+        w2_codes = keep.tile([P, N], U32, name="w2_codes", tag="centred_then_codes", align_bytes=64)
+        w2_plane = keep.tile([P, N], U8, name="w2_plane", align_bytes=64)
+        nc.vector.quantize_mx(out=w2_codes[:].bitcast(FP8X4), scales=w2_plane[:], in_=w2_bf[:].rearrange("p n t -> p (n t)"))
 
         z_bf = [keep.tile([P, width, PACK], BF16, name=f"z_bf{c}", align_bytes=64) for c, (first, width) in enumerate(CHUNKS)]
 

@@ -26,7 +26,8 @@ SCALE_ROW0 = P - K // 32
 RUN = BANK // 2
 NEIGHBOURS = 4
 CHUNKS = ((0, 256), (256, 256), (512, 256), (768, 128), (896, 128))
-SCALAR_TAIL = 48
+SCALAR_TAIL = 64
+COPIED = 0
 
 
 def tile_picked_inorm_none_p_kernel(tc, x_words, x_scales, w1, w2, gamma, offs, out):
@@ -57,9 +58,9 @@ def tile_picked_inorm_none_p_kernel(tc, x_words, x_scales, w1, w2, gamma, offs, 
         nc.vector.memset(warm[:], 1.0)
         nc.scalar.activation(warm_out[:], warm[:], ACT.Abs_reciprocal_sqrt)
 
-        stats = {t: keep.tile([P, HALVES, 2, 3], F32, name=f"stats{t}") for t in (0, 2, 3)}
+        stats = {t: keep.tile([P, HALVES, 2, 3], F32, name=f"stats{t}") for t in range(1, PACK)}
 
-        terms = keep.tile([P, PACK, 2, 6], F32, name="terms")
+        terms = keep.tile([P, PACK - 1, 2, 6], F32, name="terms")
         nc.vector.memset(terms[:, :, 0, 0], -1.0)
 
         nc.vector.tensor_copy(picked_scales[:], table_scales[:].indirect(offsets[:]))
@@ -97,7 +98,7 @@ def tile_picked_inorm_none_p_kernel(tc, x_words, x_scales, w1, w2, gamma, offs, 
                 stop=True,
             )
 
-        w1_bf = keep.tile([P, PACK, P, PACK], BF16, name="w1_bf", tag="dealt_weights", align_bytes=64)
+        w1_bf = keep.tile([P, PACK, P, PACK], BF16, name="w1_bf", align_bytes=64)
 
         def deal_w1(copy, raw, j0, m0, m1, t0, t1):
             src = raw.rearrange("p e (m t) -> p m e t", t=PACK)[:, :, :, t0:t1]
@@ -106,27 +107,27 @@ def tile_picked_inorm_none_p_kernel(tc, x_words, x_scales, w1, w2, gamma, offs, 
 
         deal_w1(nc.scalar.copy, w1_first[:], 0, 0, P // 2, 0, PACK)
         deal_w1(nc.scalar.copy, w1_second, 0, P // 2, P, 0, PACK)
-        deal_w1(nc.vector.tensor_copy, w1_third, 2, 0, P, 0, 1)
         deal_w1(nc.vector.tensor_copy, w1_third, 2, 0, P, 1, 2)
+        deal_w1(nc.vector.tensor_copy, w1_third, 2, 0, P, 0, 1)
         deal_w1(nc.scalar.copy, w1_third, 2, 0, P, 2, 4)
 
-        w1_codes = [keep.tile([P, P], U32, name=f"w1_codes{t}", align_bytes=64) for t in range(PACK)]
-        w1_plane = [keep.tile([P, P], U8, name=f"w1_plane{t}", align_bytes=64) for t in range(PACK)]
-        for t in range(PACK):
-            nc.vector.quantize_mx(out=w1_codes[t][:].bitcast(FP8X4), scales=w1_plane[t][:], in_=w1_bf[:, t].rearrange("p m j -> p (m j)"))
+        codes = keep.tile([P, PACK * P], U32, name="w1_codes", align_bytes=64)
+        plane = keep.tile([P, PACK * P], U8, name="w1_plane", align_bytes=64)
+        w1_codes = [codes[:, t * P : (t + 1) * P] for t in range(PACK)]
+        w1_plane = [plane[:, t * P : (t + 1) * P] for t in range(PACK)]
+        for t0, t1 in ((1, 2), (0, 1), (2, 4)):
+            nc.vector.quantize_mx(out=codes[:, t0 * P : t1 * P].bitcast(FP8X4), scales=plane[:, t0 * P : t1 * P], in_=w1_bf[:, t0:t1].rearrange("p t m j -> p (t m j)"))
 
-        nc.scalar.activation(terms[:, :, :, 4], gain.unsqueeze(2).to_broadcast([P, PACK, 2]), ACT.Identity, scale=-1.0)
+        nc.scalar.activation(terms[:, :, :, 4], gain[:, 1:PACK].unsqueeze(2).to_broadcast([P, PACK - 1, 2]), ACT.Identity, scale=-1.0)
 
-        z_all = keep.tile([P, HALVES, PACK, BANK], BF16, name="z_all", align_bytes=64)
-        z_rows = [z_all[:, s] for s in range(HALVES)]
         affine = {}
 
         def product(t, s):
             for c0 in range(0, BANK, RUN):
                 nc.tensor.matmul_mx(
                     out=h[t, s][:, c0 : c0 + RUN],
-                    lhsT=w1_codes[t][:].bitcast(FP8X4),
-                    lhsT_scale=w1_plane[t][:],
+                    lhsT=w1_codes[t].bitcast(FP8X4),
+                    lhsT_scale=w1_plane[t],
                     rhs=x_codes[s][:, c0 : c0 + RUN].bitcast(FP8X4),
                     rhs_scale=x_plane[:, s * BANK + c0 : s * BANK + c0 + RUN],
                     start=True,
@@ -136,27 +137,11 @@ def tile_picked_inorm_none_p_kernel(tc, x_words, x_scales, w1, w2, gamma, offs, 
         def stats_on_vector(t, s):
             nc.vector.bn_stats(stats[t][:, s].rearrange("p r e -> p (r e)"), h[t, s][:])
 
-        scaled_h = keep.tile([P, S], F32, name="scaled_h")
-
-        def stats_on_scalar(t):
-            part = keep.tile([P, HALVES], F32, name="part")
-            for s in range(HALVES):
-                nc.scalar.activation(scaled_h[:, s * BANK : (s + 1) * BANK], h[t, s][:], ACT.Identity, scale=1.0 / S, accum_out=part[:, s : s + 1])
-            nc.scalar.activation(terms[:, t, 1, 0:1], part[:, 0:1], ACT.Identity, bias=part[:, 1:2])
-            centred = keep.tile([P, S], F32, name="centred", tag="centred_then_codes", align_bytes=64)
-            nc.gpsimd.tensor_scalar(centred[:], scaled_h[:], -float(S), terms[:, t, 1, 0:1], ALU.mult, ALU.add)
-            spent = z_all[:, :, 0, :]
-            squares = terms[:, t, 1, 1:2]
-            nc.scalar.activation(spent, scaled_h[:].rearrange("p (s n) -> p s n", s=HALVES), ACT.Square, scale=-float(S), bias=terms[:, t, 1, 0:1], accum_out=squares)
-            rstd = keep.tile([P, 1], F32, name=f"rstd{t}")
-            nc.scalar.activation(rstd[:], squares, ACT.Abs_reciprocal_sqrt, scale=1.0 / S, bias=EPS)
-            nc.gpsimd.tensor_scalar(z_all[:, :, t, :], centred[:].rearrange("p (s n) -> p s n", s=HALVES), rstd[:], terms[:, t, 0, 4:5], ALU.mult, ALU.mult)
-
         def affine_of(t):
-            nc.vector.bn_aggr(terms[:, t, 1, 0:2], stats[t][:].rearrange("p s r e -> p (s r e)"))
-            nc.scalar.activation(terms[:, t, :, 2], terms[:, t, 1, 1:2].to_broadcast([P, 2]), ACT.Abs_reciprocal_sqrt, bias=EPS)
+            nc.vector.bn_aggr(terms[:, t - 1, 1, 0:2], stats[t][:].rearrange("p s r e -> p (s r e)"))
+            nc.scalar.activation(terms[:, t - 1, :, 2], terms[:, t - 1, 1, 1:2].to_broadcast([P, 2]), ACT.Abs_reciprocal_sqrt, bias=EPS)
             affine[t] = keep.tile([P, 2], F32, name=f"affine{t}")
-            nc.vector.tensor_reduce(affine[t][:], terms[:, t, :, 0:6:2], mybir.AxisListType.X, ALU.mult)
+            nc.vector.tensor_reduce(affine[t][:], terms[:, t - 1, :, 0:6:2], mybir.AxisListType.X, ALU.mult)
 
         def normalise_on_scalar(t, s):
             nc.scalar.activation(z_rows[s][:, t, :], h[t, s][:], ACT.Identity, bias=affine[t][:, 1:2], scale=affine[t][:, 0:1])
@@ -164,16 +149,33 @@ def tile_picked_inorm_none_p_kernel(tc, x_words, x_scales, w1, w2, gamma, offs, 
         def normalise_on_vector(t, s, c0, c1):
             nc.vector.tensor_scalar(z_rows[s][:, t, c0:c1], h[t, s][:, c0:c1], affine[t][:, 0:1], affine[t][:, 1:2], ALU.mult, ALU.add)
 
-        for pair in ((0, 1), (2,), (3,)):
+        for pair in ((1, COPIED), (2,), (3,)):
             for s in range(HALVES):
                 for t in pair:
                     product(t, s)
         w2_bf = keep.tile([P, N, PACK], BF16, name="w2_bf", align_bytes=64)
         nc.scalar.copy(w2_bf[:].rearrange("p (c i) t -> p c t i", i=NEIGHBOURS), w2_raw.rearrange("p t (c i) -> p c t i", i=NEIGHBOURS))
         for s in range(HALVES):
-            stats_on_vector(0, s)
-        affine_of(0)
-        stats_on_scalar(1)
+            stats_on_vector(1, s)
+        affine_of(1)
+
+        scaled_h = keep.tile([P, S], F32, name="scaled_h", tag="copy_then_rows", align_bytes=64)
+        part = keep.tile([P, HALVES], F32, name="part")
+        minus_mean = keep.tile([P, 1], F32, name="minus_mean")
+        squares = keep.tile([P, 1], F32, name="squares")
+        spent = keep.tile([P, S], BF16, name="spent")
+        rstd = keep.tile([P, 1], F32, name="rstd")
+        centred = keep.tile([P, S], F32, name="centred", tag="centred_then_codes", align_bytes=64)
+        for s in range(HALVES):
+            nc.scalar.activation(scaled_h[:, s * BANK : (s + 1) * BANK], h[COPIED, s][:], ACT.Identity, scale=-1.0 / S, accum_out=part[:, s : s + 1])
+        nc.scalar.activation(minus_mean[:], part[:, 0:1], ACT.Identity, bias=part[:, 1:2])
+        nc.gpsimd.tensor_scalar(centred[:], scaled_h[:], -float(S), minus_mean[:], ALU.mult, ALU.add)
+        nc.scalar.activation(spent[:], scaled_h[:], ACT.Square, scale=-float(S), bias=minus_mean[:], accum_out=squares[:])
+        nc.scalar.activation(rstd[:], squares[:], ACT.Abs_reciprocal_sqrt, scale=1.0 / S, bias=EPS)
+        z_all = keep.tile([P, HALVES, PACK, BANK], BF16, name="z_all", tag="copy_then_rows", align_bytes=64)
+        z_rows = [z_all[:, s] for s in range(HALVES)]
+        nc.gpsimd.tensor_scalar(z_all[:, :, COPIED, :], centred[:].rearrange("p (s n) -> p s n", s=HALVES), rstd[:], gain[:, COPIED : COPIED + 1], ALU.mult, ALU.mult)
+
         for t in (2, 3):
             for s in range(HALVES):
                 stats_on_vector(t, s)
@@ -181,9 +183,8 @@ def tile_picked_inorm_none_p_kernel(tc, x_words, x_scales, w1, w2, gamma, offs, 
 
 
         for s in range(HALVES):
-            normalise_on_scalar(0, s)
-        for first, width in CHUNKS[:2]:
-            normalise_on_vector(2, 0, first, first + width)
+            normalise_on_scalar(1, s)
+        normalise_on_vector(2, 0, 0, BANK)
         normalise_on_scalar(2, 1)
         for first, width in CHUNKS[:2]:
             normalise_on_vector(3, 0, first, first + width)

@@ -155,8 +155,11 @@ def tile_picked_inorm_none_p_kernel(tc, x_words, x_scales, w1, w2, gamma, offs, 
                     product(t, s)
         w2_bf = keep.tile([P, N, PACK], BF16, name="w2_bf", align_bytes=64)
         nc.scalar.copy(w2_bf[:].rearrange("p (c i) t -> p c t i", i=NEIGHBOURS), w2_raw.rearrange("p t (c i) -> p c t i", i=NEIGHBOURS))
-        for s in range(HALVES):
-            stats_on_vector(1, s)
+        w2_codes = keep.tile([P, N], U32, name="w2_codes", align_bytes=64)
+        w2_plane = keep.tile([P, N], U8, name="w2_plane", align_bytes=64)
+        stats_on_vector(1, 0)
+        nc.vector.quantize_mx(out=w2_codes[:].bitcast(FP8X4), scales=w2_plane[:], in_=w2_bf[:].rearrange("p n t -> p (n t)"))
+        stats_on_vector(1, 1)
         affine_of(1)
 
         scaled_h = keep.tile([P, S], F32, name="scaled_h", tag="copy_then_rows", align_bytes=64)
@@ -165,7 +168,7 @@ def tile_picked_inorm_none_p_kernel(tc, x_words, x_scales, w1, w2, gamma, offs, 
         squares = keep.tile([P, 1], F32, name="squares")
         spent = keep.tile([P, S], BF16, name="spent")
         rstd = keep.tile([P, 1], F32, name="rstd")
-        centred = keep.tile([P, S], F32, name="centred", tag="centred_then_codes", align_bytes=64)
+        centred = keep.tile([P, S], F32, name="centred")
         for s in range(HALVES):
             nc.scalar.activation(scaled_h[:, s * BANK : (s + 1) * BANK], h[COPIED, s][:], ACT.Identity, scale=-1.0 / S, accum_out=part[:, s : s + 1])
         nc.scalar.activation(minus_mean[:], part[:, 0:1], ACT.Identity, bias=part[:, 1:2])
@@ -189,10 +192,6 @@ def tile_picked_inorm_none_p_kernel(tc, x_words, x_scales, w1, w2, gamma, offs, 
         for first, width in CHUNKS[:2]:
             normalise_on_vector(3, 0, first, first + width)
         normalise_on_scalar(3, 1)
-
-        w2_codes = keep.tile([P, N], U32, name="w2_codes", tag="centred_then_codes", align_bytes=64)
-        w2_plane = keep.tile([P, N], U8, name="w2_plane", align_bytes=64)
-        nc.vector.quantize_mx(out=w2_codes[:].bitcast(FP8X4), scales=w2_plane[:], in_=w2_bf[:].rearrange("p n t -> p (n t)"))
 
         z_bf = [keep.tile([P, width, PACK], BF16, name=f"z_bf{c}", align_bytes=64) for c, (first, width) in enumerate(CHUNKS)]
 

@@ -62,6 +62,8 @@ def tile_picked_inorm_none_p_kernel(tc, x_words, x_scales, w1, w2, gamma, offs, 
 
         terms = keep.tile([P, PACK - 1, 2, 6], F32, name="terms")
         nc.vector.memset(terms[:, :, 0, 0], -1.0)
+        copy_terms = keep.tile([P, 2], F32, name="copy_terms")
+        nc.vector.memset(copy_terms[:, 0:1], -float(S))
 
         nc.vector.tensor_copy(picked_scales[:], table_scales[:].indirect(offsets[:]))
         for q in range(P // QUADRANT):
@@ -162,22 +164,22 @@ def tile_picked_inorm_none_p_kernel(tc, x_words, x_scales, w1, w2, gamma, offs, 
         stats_on_vector(1, 1)
         affine_of(1)
 
-        scaled_h = keep.tile([P, S], F32, name="scaled_h", tag="copy_then_rows", align_bytes=64)
+        scaled_h = keep.tile([P, S], F32, name="scaled_h")
         part = keep.tile([P, HALVES], F32, name="part")
-        minus_mean = keep.tile([P, 1], F32, name="minus_mean")
+        minus_mean = keep.tile([P, 1], F32, name="minus_mean", tag="mean_then_rows", align_bytes=64)
         squares = keep.tile([P, 1], F32, name="squares")
         spent = keep.tile([P, S], BF16, name="spent")
         rstd = keep.tile([P, 1], F32, name="rstd")
-        centred = keep.tile([P, S], F32, name="centred")
         for s in range(HALVES):
             nc.scalar.activation(scaled_h[:, s * BANK : (s + 1) * BANK], h[COPIED, s][:], ACT.Identity, scale=-1.0 / S, accum_out=part[:, s : s + 1])
-        nc.scalar.activation(minus_mean[:], part[:, 0:1], ACT.Identity, bias=part[:, 1:2])
-        nc.gpsimd.tensor_scalar(centred[:], scaled_h[:], -float(S), minus_mean[:], ALU.mult, ALU.add)
+        nc.scalar.activation(minus_mean[:], part[:, 0:1], ACT.Identity, bias=part[:, 1:2], accum_out=copy_terms[:, 1:2])
         nc.scalar.activation(spent[:], scaled_h[:], ACT.Square, scale=-float(S), bias=minus_mean[:], accum_out=squares[:])
         nc.scalar.activation(rstd[:], squares[:], ACT.Abs_reciprocal_sqrt, scale=1.0 / S, bias=EPS)
-        z_all = keep.tile([P, HALVES, PACK, BANK], BF16, name="z_all", tag="copy_then_rows", align_bytes=64)
+        z_all = keep.tile([P, HALVES, PACK, BANK], BF16, name="z_all", tag="mean_then_rows", align_bytes=64)
         z_rows = [z_all[:, s] for s in range(HALVES)]
-        nc.gpsimd.tensor_scalar(z_all[:, :, COPIED, :], centred[:].rearrange("p (s n) -> p s n", s=HALVES), rstd[:], gain[:, COPIED : COPIED + 1], ALU.mult, ALU.mult)
+        affine[COPIED] = keep.tile([P, 2], F32, name="copy_affine")
+        nc.gpsimd.tensor_scalar(affine[COPIED][:], copy_terms[:], rstd[:], gain[:, COPIED : COPIED + 1], ALU.mult, ALU.mult)
+        nc.gpsimd.tensor_scalar(z_all[:, :, COPIED, :], scaled_h[:].rearrange("p (s n) -> p s n", s=HALVES), affine[COPIED][:, 0:1], affine[COPIED][:, 1:2], ALU.mult, ALU.add)
 
         for t in (2, 3):
             for s in range(HALVES):

@@ -113,12 +113,10 @@ def tile_picked_inorm_none_p_kernel(tc, x_words, x_scales, w1, w2, gamma, offs, 
         deal_w1(nc.vector.tensor_copy, w1_third, 2, 0, P, 0, 1)
         deal_w1(nc.scalar.copy, w1_third, 2, 0, P, 2, 4)
 
-        codes = keep.tile([P, PACK * P], U32, name="w1_codes", align_bytes=64)
-        plane = keep.tile([P, PACK * P], U8, name="w1_plane", align_bytes=64)
-        w1_codes = [codes[:, t * P : (t + 1) * P] for t in range(PACK)]
-        w1_plane = [plane[:, t * P : (t + 1) * P] for t in range(PACK)]
-        for t0, t1 in ((1, 2), (0, 1), (2, 4)):
-            nc.vector.quantize_mx(out=codes[:, t0 * P : t1 * P].bitcast(FP8X4), scales=plane[:, t0 * P : t1 * P], in_=w1_bf[:, t0:t1].rearrange("p t m j -> p (t m j)"))
+        w1_codes = [keep.tile([P, P], U32, name=f"w1_codes{t}", align_bytes=64) for t in range(PACK)]
+        w1_plane = [keep.tile([P, P], U8, name=f"w1_plane{t}", align_bytes=64) for t in range(PACK)]
+        for t in (1, 0, 2, 3):
+            nc.vector.quantize_mx(out=w1_codes[t][:].bitcast(FP8X4), scales=w1_plane[t][:], in_=w1_bf[:, t].rearrange("p m j -> p (m j)"))
 
         nc.scalar.activation(terms[:, :, :, 4], gain[:, 1:PACK].unsqueeze(2).to_broadcast([P, PACK - 1, 2]), ACT.Identity, scale=-1.0)
 
@@ -128,8 +126,8 @@ def tile_picked_inorm_none_p_kernel(tc, x_words, x_scales, w1, w2, gamma, offs, 
             for c0 in range(0, BANK, RUN):
                 nc.tensor.matmul_mx(
                     out=h[t, s][:, c0 : c0 + RUN],
-                    lhsT=w1_codes[t].bitcast(FP8X4),
-                    lhsT_scale=w1_plane[t],
+                    lhsT=w1_codes[t][:].bitcast(FP8X4),
+                    lhsT_scale=w1_plane[t][:],
                     rhs=x_codes[s][:, c0 : c0 + RUN].bitcast(FP8X4),
                     rhs_scale=x_plane[:, s * BANK + c0 : s * BANK + c0 + RUN],
                     start=True,
@@ -157,11 +155,8 @@ def tile_picked_inorm_none_p_kernel(tc, x_words, x_scales, w1, w2, gamma, offs, 
                     product(t, s)
         w2_bf = keep.tile([P, N, PACK], BF16, name="w2_bf", align_bytes=64)
         nc.scalar.copy(w2_bf[:].rearrange("p (c i) t -> p c t i", i=NEIGHBOURS), w2_raw.rearrange("p t (c i) -> p c t i", i=NEIGHBOURS))
-        w2_codes = keep.tile([P, N], U32, name="w2_codes", align_bytes=64)
-        w2_plane = keep.tile([P, N], U8, name="w2_plane", align_bytes=64)
-        stats_on_vector(1, 0)
-        nc.vector.quantize_mx(out=w2_codes[:].bitcast(FP8X4), scales=w2_plane[:], in_=w2_bf[:].rearrange("p n t -> p (n t)"))
-        stats_on_vector(1, 1)
+        for s in range(HALVES):
+            stats_on_vector(1, s)
         affine_of(1)
 
         scaled_h = keep.tile([P, S], F32, name="scaled_h")
@@ -186,10 +181,14 @@ def tile_picked_inorm_none_p_kernel(tc, x_words, x_scales, w1, w2, gamma, offs, 
                 stats_on_vector(t, s)
             affine_of(t)
 
+        w2_codes = keep.tile([P, N], U32, name="w2_codes", align_bytes=64)
+        w2_plane = keep.tile([P, N], U8, name="w2_plane", align_bytes=64)
+        nc.vector.quantize_mx(out=w2_codes[:].bitcast(FP8X4), scales=w2_plane[:], in_=w2_bf[:].rearrange("p n t -> p (n t)"))
 
         for s in range(HALVES):
             normalise_on_scalar(1, s)
-        normalise_on_vector(2, 0, 0, BANK)
+        for first, width in CHUNKS[:2]:
+            normalise_on_vector(2, 0, first, first + width)
         normalise_on_scalar(2, 1)
         for first, width in CHUNKS[:2]:
             normalise_on_vector(3, 0, first, first + width)

@@ -26,7 +26,7 @@ SCALE_ROW0 = P - K // 32
 RUN = BANK // 2
 NEIGHBOURS = 4
 CHUNKS = ((0, 256), (256, 256), (512, 256), (768, 128), (896, 128))
-SCALAR_TAIL = 64
+SCALAR_TAIL = 96
 COPIED = 0
 
 

@@ -89,11 +89,11 @@ def tile_picked_inorm_none_p_kernel(tc, x_words, x_scales, w1, w2, gamma, offs, 
             for s in range(HALVES):
                 h[t, s] = psum.tile([P, BANK], F32, name=f"h{t}_{s}", tag=f"bank{HALVES * t + s}")
 
-        for w in range(2):
+        for w in range(3):
             nc.tensor.matmul_mx(
-                out=h[PACK - 1, HALVES - 1][:],
-                lhsT=x_codes[0][:, 0:P].bitcast(FP8X4),
-                lhsT_scale=x_plane[:, 0:P],
+                out=h[PACK - 1, HALVES - 1][0:QUADRANT, :],
+                lhsT=x_codes[0][:, 0:QUADRANT].bitcast(FP8X4),
+                lhsT_scale=x_plane[:, 0:QUADRANT],
                 rhs=x_codes[0][:].bitcast(FP8X4),
                 rhs_scale=x_plane[:, 0:BANK],
                 start=True,

@@ -24,7 +24,7 @@ BANK = 512
 HALVES = S // BANK
 SCALE_ROW0 = P - K // 32
 RUN = BANK // 2
-NEIGHBOURS = 4
+NEIGHBOURS = 8
 CHUNKS = ((0, 256), (256, 256), (512, 256), (768, 128), (896, 128))
 SCALAR_TAIL = 96
 COPIED = 0

@@ -25,8 +25,9 @@ HALVES = S // BANK
 SCALE_ROW0 = P - K // 32
 RUN = BANK // 2
 NEIGHBOURS = 8
-CHUNKS = ((0, 256), (256, 256), (512, 256), (768, 128), (896, 128))
+CHUNKS = ((0, 256), (256, 256), (512, 256), (768, 128), (896, 64), (960, 64))
 SCALAR_TAIL = 96
+ROOT_S = 32.0
 COPIED = 0
 
 
@@ -35,6 +36,7 @@ def tile_picked_inorm_none_p_kernel(tc, x_words, x_scales, w1, w2, gamma, offs, 
     with ExitStack() as ctx:
         keep = ctx.enter_context(tc.tile_pool(name="keep", bufs=1))
         psum = ctx.enter_context(tc.psum_pool(name="psum", bufs=1))
+        placed = ctx.enter_context(tc.tile_pool(name="placed", bufs=1))
 
         offsets = keep.tile([P, S // GROUP], U16, name="offsets")
         table_words = keep.tile([P, T], U32, name="table_words", align_bytes=64)
@@ -60,7 +62,7 @@ def tile_picked_inorm_none_p_kernel(tc, x_words, x_scales, w1, w2, gamma, offs, 
 
         stats = {t: keep.tile([P, HALVES, 2, 3], F32, name=f"stats{t}") for t in range(1, PACK)}
 
-        terms = keep.tile([P, PACK - 1, 2, 6], F32, name="terms")
+        terms = keep.tile([P, PACK, 2, 6], F32, name="terms")
         nc.vector.memset(terms[:, :, 0, 0], -1.0)
         copy_terms = keep.tile([P, 2], F32, name="copy_terms")
         nc.vector.memset(copy_terms[:, 0:1], -float(S))
@@ -89,16 +91,19 @@ def tile_picked_inorm_none_p_kernel(tc, x_words, x_scales, w1, w2, gamma, offs, 
             for s in range(HALVES):
                 h[t, s] = psum.tile([P, BANK], F32, name=f"h{t}_{s}", tag=f"bank{HALVES * t + s}")
 
-        for w in range(3):
-            nc.tensor.matmul_mx(
-                out=h[PACK - 1, HALVES - 1][0:QUADRANT, :],
-                lhsT=x_codes[0][:, 0:QUADRANT].bitcast(FP8X4),
-                lhsT_scale=x_plane[:, 0:QUADRANT],
-                rhs=x_codes[0][:].bitcast(FP8X4),
-                rhs_scale=x_plane[:, 0:BANK],
-                start=True,
-                stop=True,
-            )
+        def warm_tensor_engine(bank):
+            for w in range(2):
+                nc.tensor.matmul_mx(
+                    out=bank[0:QUADRANT, :],
+                    lhsT=x_codes[0][:, 0:QUADRANT].bitcast(FP8X4),
+                    lhsT_scale=x_plane[:, 0:QUADRANT],
+                    rhs=x_codes[0][:].bitcast(FP8X4),
+                    rhs_scale=x_plane[:, 0:BANK],
+                    start=True,
+                    stop=True,
+                )
+
+        warm_tensor_engine(h[PACK - 1, HALVES - 1])
 
         w1_bf = keep.tile([P, PACK, P, PACK], BF16, name="w1_bf", align_bytes=64)
 
@@ -118,8 +123,6 @@ def tile_picked_inorm_none_p_kernel(tc, x_words, x_scales, w1, w2, gamma, offs, 
         for t in (1, 0, 2, 3):
             nc.vector.quantize_mx(out=w1_codes[t][:].bitcast(FP8X4), scales=w1_plane[t][:], in_=w1_bf[:, t].rearrange("p m j -> p (m j)"))
 
-        nc.scalar.activation(terms[:, :, :, 4], gain[:, 1:PACK].unsqueeze(2).to_broadcast([P, PACK - 1, 2]), ACT.Identity, scale=-1.0)
-
         affine = {}
 
         def product(t, s):
@@ -138,10 +141,15 @@ def tile_picked_inorm_none_p_kernel(tc, x_words, x_scales, w1, w2, gamma, offs, 
             nc.vector.bn_stats(stats[t][:, s].rearrange("p r e -> p (r e)"), h[t, s][:])
 
         def affine_of(t):
-            nc.vector.bn_aggr(terms[:, t - 1, 1, 0:2], stats[t][:].rearrange("p s r e -> p (s r e)"))
-            nc.scalar.activation(terms[:, t - 1, :, 2], terms[:, t - 1, 1, 1:2].to_broadcast([P, 2]), ACT.Abs_reciprocal_sqrt, bias=EPS)
+            nc.vector.bn_aggr(terms[:, t, 1, 0:2], stats[t][:].rearrange("p s r e -> p (s r e)"))
+            rooted = terms[:, COPIED : t + 1 : t - COPIED] if t == 2 else terms[:, t : t + 1]
+            count = 2 if t == 2 else 1
+            nc.scalar.activation(rooted[:, :, :, 2], rooted[:, :, 1, 1:2].to_broadcast([P, count, 2]), ACT.Abs_reciprocal_sqrt, scale=1.0 / S, bias=EPS / S)
             affine[t] = keep.tile([P, 2], F32, name=f"affine{t}")
-            nc.vector.tensor_reduce(affine[t][:], terms[:, t - 1, :, 0:6:2], mybir.AxisListType.X, ALU.mult)
+            if t == 1:
+                nc.gpsimd.tensor_scalar(affine[t][:], terms[:, t, :, 0], terms[:, t, 0, 2:3], terms[:, t, 0, 4:5], ALU.mult, ALU.mult)
+            else:
+                nc.vector.tensor_reduce(affine[t][:], terms[:, t, :, 0:6:2], mybir.AxisListType.X, ALU.mult)
 
         def normalise_on_scalar(t, s):
             nc.scalar.activation(z_rows[s][:, t, :], h[t, s][:], ACT.Identity, bias=affine[t][:, 1:2], scale=affine[t][:, 0:1])
@@ -157,29 +165,30 @@ def tile_picked_inorm_none_p_kernel(tc, x_words, x_scales, w1, w2, gamma, offs, 
         nc.scalar.copy(w2_bf[:].rearrange("p (c i) t -> p c t i", i=NEIGHBOURS), w2_raw.rearrange("p t (c i) -> p c t i", i=NEIGHBOURS))
         for s in range(HALVES):
             stats_on_vector(1, s)
-        affine_of(1)
 
         scaled_h = keep.tile([P, S], F32, name="scaled_h")
         part = keep.tile([P, HALVES], F32, name="part")
-        minus_mean = keep.tile([P, 1], F32, name="minus_mean", tag="mean_then_rows", align_bytes=64)
-        squares = keep.tile([P, 1], F32, name="squares")
+        mean_slot = placed.tile([P, 32], F32, name="mean_slot", offset=2 * PACK * BANK, align_bytes=64)
+        minus_mean = mean_slot[:, 0:1]
         spent = keep.tile([P, S], BF16, name="spent")
-        rstd = keep.tile([P, 1], F32, name="rstd")
         for s in range(HALVES):
-            nc.scalar.activation(scaled_h[:, s * BANK : (s + 1) * BANK], h[COPIED, s][:], ACT.Identity, scale=-1.0 / S, accum_out=part[:, s : s + 1])
-        nc.scalar.activation(minus_mean[:], part[:, 0:1], ACT.Identity, bias=part[:, 1:2], accum_out=copy_terms[:, 1:2])
-        nc.scalar.activation(spent[:], scaled_h[:], ACT.Square, scale=-float(S), bias=minus_mean[:], accum_out=squares[:])
-        nc.scalar.activation(rstd[:], squares[:], ACT.Abs_reciprocal_sqrt, scale=1.0 / S, bias=EPS)
-        z_all = keep.tile([P, HALVES, PACK, BANK], BF16, name="z_all", tag="mean_then_rows", align_bytes=64)
-        z_rows = [z_all[:, s] for s in range(HALVES)]
+            nc.scalar.activation(scaled_h[:, s * BANK : (s + 1) * BANK], h[COPIED, s][:], ACT.Identity, scale=-1.0 / (S * ROOT_S), accum_out=part[:, s : s + 1])
+        nc.scalar.activation(terms[:, 1:PACK, :, 4], gain[:, 1:PACK].unsqueeze(2).to_broadcast([P, PACK - 1, 2]), ACT.Identity, scale=-1.0 / ROOT_S)
+        affine_of(1)
+        nc.scalar.activation(minus_mean, part[:, 0:1], ACT.Identity, bias=part[:, 1:2], accum_out=copy_terms[:, 1:2])
+        nc.scalar.activation(spent[:], scaled_h[:], ACT.Square, scale=-float(S), bias=minus_mean, accum_out=terms[:, COPIED, 1, 1:2])
+        for s in range(HALVES):
+            stats_on_vector(2, s)
+        affine_of(2)
+        z_rows = [placed.tile([P, PACK, BANK], BF16, name=f"z_rows{s}", offset=64 + s * 2 * PACK * BANK, align_bytes=64) for s in range(HALVES)]
         affine[COPIED] = keep.tile([P, 2], F32, name="copy_affine")
-        nc.gpsimd.tensor_scalar(affine[COPIED][:], copy_terms[:], rstd[:], gain[:, COPIED : COPIED + 1], ALU.mult, ALU.mult)
-        nc.gpsimd.tensor_scalar(z_all[:, :, COPIED, :], scaled_h[:].rearrange("p (s n) -> p s n", s=HALVES), affine[COPIED][:, 0:1], affine[COPIED][:, 1:2], ALU.mult, ALU.add)
+        nc.gpsimd.tensor_scalar(affine[COPIED][:], copy_terms[:], terms[:, COPIED, 0, 2:3], gain[:, COPIED : COPIED + 1], ALU.mult, ALU.mult)
+        for s in range(HALVES):
+            nc.gpsimd.tensor_scalar(z_rows[s][:, COPIED, :], scaled_h[:, s * BANK : (s + 1) * BANK], affine[COPIED][:, 0:1], affine[COPIED][:, 1:2], ALU.mult, ALU.add)
 
-        for t in (2, 3):
-            for s in range(HALVES):
-                stats_on_vector(t, s)
-            affine_of(t)
+        for s in range(HALVES):
+            stats_on_vector(3, s)
+        affine_of(3)
 
         w2_codes = keep.tile([P, N], U32, name="w2_codes", align_bytes=64)
         w2_plane = keep.tile([P, N], U8, name="w2_plane", align_bytes=64)
@@ -193,6 +202,8 @@ def tile_picked_inorm_none_p_kernel(tc, x_words, x_scales, w1, w2, gamma, offs, 
         for first, width in CHUNKS[:2]:
             normalise_on_vector(3, 0, first, first + width)
         normalise_on_scalar(3, 1)
+
+        warm_tensor_engine(h[PACK - 1, 0])
 
         z_bf = [keep.tile([P, width, PACK], BF16, name=f"z_bf{c}", align_bytes=64) for c, (first, width) in enumerate(CHUNKS)]
 
@@ -232,15 +243,14 @@ def tile_picked_inorm_none_p_kernel(tc, x_words, x_scales, w1, w2, gamma, offs, 
                 nc.sync.dma_start(out[:, piece * RUN : (piece + 1) * RUN], result[piece][:])
 
         last = len(CHUNKS) - 1
-        for c in (1, 3):
+        for c in (1, 3, 4):
             weave(nc.scalar.copy, c, 0, CHUNKS[c][1])
-        weave(nc.scalar.copy, last, 0, SCALAR_TAIL)
         for c in (0, 2):
             weave(nc.vector.tensor_copy, c, 0, CHUNKS[c][1])
         for c in (0, 1, 2):
             second_layer(c)
-        weave(nc.vector.tensor_copy, last, SCALAR_TAIL, CHUNKS[last][1])
+        weave(nc.vector.tensor_copy, last, 0, CHUNKS[last][1])
         for c in range(3, len(CHUNKS)):
             second_layer(c)
         for c in range(len(CHUNKS)):
-            store(nc.vector.tensor_copy if c in (2, last) else nc.scalar.copy, c)
+            store(nc.vector.tensor_copy if c > 2 else nc.scalar.copy, c)

@@ -36,7 +36,6 @@ def tile_picked_inorm_none_p_kernel(tc, x_words, x_scales, w1, w2, gamma, offs, 
     with ExitStack() as ctx:
         keep = ctx.enter_context(tc.tile_pool(name="keep", bufs=1))
         psum = ctx.enter_context(tc.psum_pool(name="psum", bufs=1))
-        placed = ctx.enter_context(tc.tile_pool(name="placed", bufs=1))
 
         offsets = keep.tile([P, S // GROUP], U16, name="offsets")
         table_words = keep.tile([P, T], U32, name="table_words", align_bytes=64)
@@ -91,8 +90,8 @@ def tile_picked_inorm_none_p_kernel(tc, x_words, x_scales, w1, w2, gamma, offs, 
             for s in range(HALVES):
                 h[t, s] = psum.tile([P, BANK], F32, name=f"h{t}_{s}", tag=f"bank{HALVES * t + s}")
 
-        def warm_tensor_engine(bank):
-            for w in range(2):
+        def warm_tensor_engine(bank, passes):
+            for w in range(passes):
                 nc.tensor.matmul_mx(
                     out=bank[0:QUADRANT, :],
                     lhsT=x_codes[0][:, 0:QUADRANT].bitcast(FP8X4),
@@ -103,7 +102,7 @@ def tile_picked_inorm_none_p_kernel(tc, x_words, x_scales, w1, w2, gamma, offs, 
                     stop=True,
                 )
 
-        warm_tensor_engine(h[PACK - 1, HALVES - 1])
+        warm_tensor_engine(h[PACK - 1, HALVES - 1], 3)
 
         w1_bf = keep.tile([P, PACK, P, PACK], BF16, name="w1_bf", align_bytes=64)
 
@@ -168,8 +167,8 @@ def tile_picked_inorm_none_p_kernel(tc, x_words, x_scales, w1, w2, gamma, offs, 
 
         scaled_h = keep.tile([P, S], F32, name="scaled_h")
         part = keep.tile([P, HALVES], F32, name="part")
-        mean_slot = placed.tile([P, 32], F32, name="mean_slot", offset=2 * PACK * BANK, align_bytes=64)
-        minus_mean = mean_slot[:, 0:1]
+        mean_slot = keep.tile([P, 1], F32, name="minus_mean", tag="mean_then_rows", align_bytes=64)
+        minus_mean = mean_slot[:]
         spent = keep.tile([P, S], BF16, name="spent")
         for s in range(HALVES):
             nc.scalar.activation(scaled_h[:, s * BANK : (s + 1) * BANK], h[COPIED, s][:], ACT.Identity, scale=-1.0 / (S * ROOT_S), accum_out=part[:, s : s + 1])
@@ -180,11 +179,11 @@ def tile_picked_inorm_none_p_kernel(tc, x_words, x_scales, w1, w2, gamma, offs, 
         for s in range(HALVES):
             stats_on_vector(2, s)
         affine_of(2)
-        z_rows = [placed.tile([P, PACK, BANK], BF16, name=f"z_rows{s}", offset=64 + s * 2 * PACK * BANK, align_bytes=64) for s in range(HALVES)]
+        z_all = keep.tile([P, HALVES, PACK, BANK], BF16, name="z_all", tag="mean_then_rows", align_bytes=64)
+        z_rows = [z_all[:, s] for s in range(HALVES)]
         affine[COPIED] = keep.tile([P, 2], F32, name="copy_affine")
         nc.gpsimd.tensor_scalar(affine[COPIED][:], copy_terms[:], terms[:, COPIED, 0, 2:3], gain[:, COPIED : COPIED + 1], ALU.mult, ALU.mult)
-        for s in range(HALVES):
-            nc.gpsimd.tensor_scalar(z_rows[s][:, COPIED, :], scaled_h[:, s * BANK : (s + 1) * BANK], affine[COPIED][:, 0:1], affine[COPIED][:, 1:2], ALU.mult, ALU.add)
+        nc.gpsimd.tensor_scalar(z_all[:, :, COPIED, :], scaled_h[:].rearrange("p (s n) -> p s n", s=HALVES), affine[COPIED][:, 0:1], affine[COPIED][:, 1:2], ALU.mult, ALU.add)
 
         for s in range(HALVES):
             stats_on_vector(3, s)
@@ -203,7 +202,7 @@ def tile_picked_inorm_none_p_kernel(tc, x_words, x_scales, w1, w2, gamma, offs, 
             normalise_on_vector(3, 0, first, first + width)
         normalise_on_scalar(3, 1)
 
-        warm_tensor_engine(h[PACK - 1, 0])
+        warm_tensor_engine(h[PACK - 1, 0], 1)
 
         z_bf = [keep.tile([P, width, PACK], BF16, name=f"z_bf{c}", align_bytes=64) for c, (first, width) in enumerate(CHUNKS)]
 

@@ -202,8 +202,6 @@ def tile_picked_inorm_none_p_kernel(tc, x_words, x_scales, w1, w2, gamma, offs, 
             normalise_on_vector(3, 0, first, first + width)
         normalise_on_scalar(3, 1)
 
-        warm_tensor_engine(h[PACK - 1, 0], 1)
-
         z_bf = [keep.tile([P, width, PACK], BF16, name=f"z_bf{c}", align_bytes=64) for c, (first, width) in enumerate(CHUNKS)]
 
         def weave(copy, c, n0, n1):

@@ -41,6 +41,8 @@ def tile_picked_inorm_none_p_kernel(tc, x_words, x_scales, w1, w2, gamma, offs, 
         table_words = keep.tile([P, T], U32, name="table_words", align_bytes=64)
         table_scales = keep.tile([P, T], U8, name="table_scales", tag="scales_then_weights", align_bytes=64)
         w1_first = keep.tile([P, 2, H // 2], F32, name="w1_first")
+        w1_second = keep.tile([P, 2, H // 2], F32, name="w1_second")
+        w1_third = keep.tile([P, 2, H], F32, name="w1_third")
         x_codes = [keep.tile([P, BANK], U32, name=f"x_codes{s}", align_bytes=64) for s in range(HALVES)]
         picked_scales = keep.tile([P, S], U8, name="picked_scales", align_bytes=64)
         x_plane = keep.tile([P, S], U8, name="x_plane", align_bytes=64)
@@ -53,33 +55,30 @@ def tile_picked_inorm_none_p_kernel(tc, x_words, x_scales, w1, w2, gamma, offs, 
         nc.sync.dma_start(table_words[:].bitcast(I32), x_words[0].rearrange("p n t -> p (n t)").bitcast(I32))
         w1_rows = w1.rearrange("(p j) c -> p j c", j=PACK)
         nc.sync.dma_start(w1_first[:], w1_rows[:, 0:2, 0 : H // 2])
+        nc.sync.dma_start(w1_second[:], w1_rows[:, 0:2, H // 2 : H])
+        nc.sync.dma_start(w1_third[:], w1_rows[:, 2:4, :])
 
         warm = keep.tile([P, 1], F32, name="warm")
         warm_out = keep.tile([P, 1], F32, name="warm_out")
         nc.vector.memset(warm[:], 1.0)
         nc.scalar.activation(warm_out[:], warm[:], ACT.Abs_reciprocal_sqrt)
 
-        stats = {t: keep.tile([P, HALVES, 2, 3], F32, name=f"stats{t}") for t in range(1, PACK)}
+        stats = {t: keep.tile([P, HALVES, 2, 3], F32, name=f"stats{t}", tag=f"stats{t}", align_bytes=64) for t in range(1, PACK)}
 
-        terms = keep.tile([P, PACK, 2, 6], F32, name="terms")
-        nc.vector.memset(terms[:, :, 0, 0], -1.0)
+        terms = keep.tile([P, 3, PACK, 4], F32, name="terms")
+        nc.vector.memset(terms[:, 0, 1:PACK, 0], -1.0)
         copy_terms = keep.tile([P, 2], F32, name="copy_terms")
         nc.vector.memset(copy_terms[:, 0:1], -float(S))
 
         nc.vector.tensor_copy(picked_scales[:], table_scales[:].indirect(offsets[:]))
         for q in range(P // QUADRANT):
-            queue = nc.sync if q % 2 == 0 else nc.scalar
-            queue.dma_start(
+            nc.sync.dma_start(
                 x_plane[QUADRANT * q : QUADRANT * q + 4, :].bitcast(I32),
                 picked_scales[SCALE_ROW0 + 4 * q : SCALE_ROW0 + 4 * q + 4, :].bitcast(I32),
             )
-        late_weights = keep.tile([P, 3 * H + PACK * N + PACK], F32, name="late_weights", tag="scales_then_weights", align_bytes=64)
-        w1_second = late_weights[:, 0:H].rearrange("p (e c) -> p e c", e=2)
-        w1_third = late_weights[:, H : 3 * H].rearrange("p (e c) -> p e c", e=2)
-        w2_raw = late_weights[:, 3 * H : 3 * H + PACK * N].rearrange("p (t n) -> p t n", t=PACK)
-        gain = late_weights[:, 3 * H + PACK * N :]
-        nc.sync.dma_start(w1_second, w1_rows[:, 0:2, H // 2 : H])
-        nc.sync.dma_start(w1_third, w1_rows[:, 2:4, :])
+        late_weights = keep.tile([P, PACK * N + PACK], F32, name="late_weights", tag="scales_then_weights", align_bytes=64)
+        w2_raw = late_weights[:, 0 : PACK * N].rearrange("p (t n) -> p t n", t=PACK)
+        gain = late_weights[:, PACK * N :]
         nc.sync.dma_start(w2_raw, w2.rearrange("(p t) n -> p t n", t=PACK))
         nc.sync.dma_start(gain, gamma.rearrange("(p t) o -> p (t o)", t=PACK))
         for s in range(HALVES):
@@ -95,16 +94,16 @@ def tile_picked_inorm_none_p_kernel(tc, x_words, x_scales, w1, w2, gamma, offs, 
                 nc.tensor.matmul_mx(
                     out=bank[0:QUADRANT, :],
                     lhsT=x_codes[0][:, 0:QUADRANT].bitcast(FP8X4),
-                    lhsT_scale=x_plane[:, 0:QUADRANT],
+                    lhsT_scale=picked_scales[:, 0:QUADRANT],
                     rhs=x_codes[0][:].bitcast(FP8X4),
-                    rhs_scale=x_plane[:, 0:BANK],
+                    rhs_scale=picked_scales[:, 0:BANK],
                     start=True,
                     stop=True,
                 )
 
         warm_tensor_engine(h[PACK - 1, HALVES - 1], 3)
 
-        w1_bf = keep.tile([P, PACK, P, PACK], BF16, name="w1_bf", align_bytes=64)
+        w1_bf = keep.tile([P, PACK, P, PACK], BF16, name="w1_bf", tag="dealt", align_bytes=64)
 
         def deal_w1(copy, raw, j0, m0, m1, t0, t1):
             src = raw.rearrange("p e (m t) -> p m e t", t=PACK)[:, :, :, t0:t1]
@@ -112,10 +111,10 @@ def tile_picked_inorm_none_p_kernel(tc, x_words, x_scales, w1, w2, gamma, offs, 
             copy(dst, src)
 
         deal_w1(nc.scalar.copy, w1_first[:], 0, 0, P // 2, 0, PACK)
-        deal_w1(nc.scalar.copy, w1_second, 0, P // 2, P, 0, PACK)
-        deal_w1(nc.vector.tensor_copy, w1_third, 2, 0, P, 1, 2)
-        deal_w1(nc.vector.tensor_copy, w1_third, 2, 0, P, 0, 1)
-        deal_w1(nc.scalar.copy, w1_third, 2, 0, P, 2, 4)
+        deal_w1(nc.scalar.copy, w1_second[:], 0, P // 2, P, 0, PACK)
+        deal_w1(nc.vector.tensor_copy, w1_third[:], 2, 0, P, 1, 2)
+        deal_w1(nc.vector.tensor_copy, w1_third[:], 2, 0, P, 0, 1)
+        deal_w1(nc.scalar.copy, w1_third[:], 2, 0, P, 2, 4)
 
         w1_codes = [keep.tile([P, P], U32, name=f"w1_codes{t}", align_bytes=64) for t in range(PACK)]
         w1_plane = [keep.tile([P, P], U8, name=f"w1_plane{t}", align_bytes=64) for t in range(PACK)]
@@ -140,15 +139,15 @@ def tile_picked_inorm_none_p_kernel(tc, x_words, x_scales, w1, w2, gamma, offs, 
             nc.vector.bn_stats(stats[t][:, s].rearrange("p r e -> p (r e)"), h[t, s][:])
 
         def affine_of(t):
-            nc.vector.bn_aggr(terms[:, t, 1, 0:2], stats[t][:].rearrange("p s r e -> p (s r e)"))
-            rooted = terms[:, COPIED : t + 1 : t - COPIED] if t == 2 else terms[:, t : t + 1]
+            nc.vector.bn_aggr(terms[:, 0, t, 1:3], stats[t][:].rearrange("p s r e -> p (s r e)"))
+            tiles = slice(COPIED, t + 1, t - COPIED) if t == 2 else slice(t, t + 1)
             count = 2 if t == 2 else 1
-            nc.scalar.activation(rooted[:, :, :, 2], rooted[:, :, 1, 1:2].to_broadcast([P, count, 2]), ACT.Abs_reciprocal_sqrt, scale=1.0 / S, bias=EPS / S)
+            nc.scalar.activation(terms[:, 1, tiles, 0:2], terms[:, 0, tiles, 2:3].to_broadcast([P, count, 2]), ACT.Abs_reciprocal_sqrt, scale=1.0 / S, bias=EPS / S)
             affine[t] = keep.tile([P, 2], F32, name=f"affine{t}")
             if t == 1:
-                nc.gpsimd.tensor_scalar(affine[t][:], terms[:, t, :, 0], terms[:, t, 0, 2:3], terms[:, t, 0, 4:5], ALU.mult, ALU.mult)
+                nc.gpsimd.tensor_scalar(affine[t][:], terms[:, 0, t, 0:2], terms[:, 1, t, 0:1], terms[:, 2, t, 0:1], ALU.mult, ALU.mult)
             else:
-                nc.vector.tensor_reduce(affine[t][:], terms[:, t, :, 0:6:2], mybir.AxisListType.X, ALU.mult)
+                nc.vector.tensor_reduce(affine[t][:], terms[:, :, t, 0:2].rearrange("p f i -> p i f"), mybir.AxisListType.X, ALU.mult)
 
         def normalise_on_scalar(t, s):
             nc.scalar.activation(z_rows[s][:, t, :], h[t, s][:], ACT.Identity, bias=affine[t][:, 1:2], scale=affine[t][:, 0:1])
@@ -160,8 +159,8 @@ def tile_picked_inorm_none_p_kernel(tc, x_words, x_scales, w1, w2, gamma, offs, 
             for s in range(HALVES):
                 for t in pair:
                     product(t, s)
-        w2_bf = keep.tile([P, N, PACK], BF16, name="w2_bf", align_bytes=64)
-        nc.scalar.copy(w2_bf[:].rearrange("p (c i) t -> p c t i", i=NEIGHBOURS), w2_raw.rearrange("p t (c i) -> p c t i", i=NEIGHBOURS))
+        w2_bf = keep.tile([P, N, PACK], BF16, name="w2_bf", tag="dealt", align_bytes=64)
+        nc.gpsimd.tensor_scalar(w2_bf[:], w2_raw.rearrange("p t n -> p n t"), 1.0, 0.0, ALU.mult, ALU.add)
         for s in range(HALVES):
             stats_on_vector(1, s)
 
@@ -172,24 +171,24 @@ def tile_picked_inorm_none_p_kernel(tc, x_words, x_scales, w1, w2, gamma, offs, 
         spent = keep.tile([P, S], BF16, name="spent")
         for s in range(HALVES):
             nc.scalar.activation(scaled_h[:, s * BANK : (s + 1) * BANK], h[COPIED, s][:], ACT.Identity, scale=-1.0 / (S * ROOT_S), accum_out=part[:, s : s + 1])
-        nc.scalar.activation(terms[:, 1:PACK, :, 4], gain[:, 1:PACK].unsqueeze(2).to_broadcast([P, PACK - 1, 2]), ACT.Identity, scale=-1.0 / ROOT_S)
+        nc.gpsimd.tensor_scalar(terms[:, 2, 1:PACK, 0:2], gain[:, 1:PACK].unsqueeze(2).to_broadcast([P, PACK - 1, 2]), -1.0 / ROOT_S, 0.0, ALU.mult, ALU.add)
         affine_of(1)
         nc.scalar.activation(minus_mean, part[:, 0:1], ACT.Identity, bias=part[:, 1:2], accum_out=copy_terms[:, 1:2])
-        nc.scalar.activation(spent[:], scaled_h[:], ACT.Square, scale=-float(S), bias=minus_mean, accum_out=terms[:, COPIED, 1, 1:2])
+        nc.scalar.activation(spent[:], scaled_h[:], ACT.Square, scale=-float(S), bias=minus_mean, accum_out=terms[:, 0, COPIED, 2:3])
         for s in range(HALVES):
             stats_on_vector(2, s)
         affine_of(2)
         z_all = keep.tile([P, HALVES, PACK, BANK], BF16, name="z_all", tag="mean_then_rows", align_bytes=64)
         z_rows = [z_all[:, s] for s in range(HALVES)]
         affine[COPIED] = keep.tile([P, 2], F32, name="copy_affine")
-        nc.gpsimd.tensor_scalar(affine[COPIED][:], copy_terms[:], terms[:, COPIED, 0, 2:3], gain[:, COPIED : COPIED + 1], ALU.mult, ALU.mult)
+        nc.gpsimd.tensor_scalar(affine[COPIED][:], copy_terms[:], terms[:, 1, COPIED, 0:1], gain[:, COPIED : COPIED + 1], ALU.mult, ALU.mult)
         nc.gpsimd.tensor_scalar(z_all[:, :, COPIED, :], scaled_h[:].rearrange("p (s n) -> p s n", s=HALVES), affine[COPIED][:, 0:1], affine[COPIED][:, 1:2], ALU.mult, ALU.add)
 
         for s in range(HALVES):
             stats_on_vector(3, s)
         affine_of(3)
 
-        w2_codes = keep.tile([P, N], U32, name="w2_codes", align_bytes=64)
+        w2_codes = keep.tile([P, N], U32, name="w2_codes", tag="stats2", align_bytes=64)
         w2_plane = keep.tile([P, N], U8, name="w2_plane", align_bytes=64)
         nc.vector.quantize_mx(out=w2_codes[:].bitcast(FP8X4), scales=w2_plane[:], in_=w2_bf[:].rearrange("p n t -> p (n t)"))
 

from contextlib import ExitStack

import concourse.mybir as mybir

K, T, S, H, N = 512, 4096, 1024, 512, 128
FLOPS = 2 * K * H * S + 2 * H * N * S
EPS = 1e-5

F32 = mybir.dt.float32
BF16 = mybir.dt.bfloat16
I32 = mybir.dt.int32
U32 = mybir.dt.uint32
U16 = mybir.dt.uint16
U8 = mybir.dt.uint8
FP8X4 = mybir.dt.float8_e4m3fn_x4
ACT = mybir.ActivationFunctionType
ALU = mybir.AluOpType

P = 128
PACK = 4
QUADRANT = 32
GROUP = 16
BANK = 512
HALVES = S // BANK
SCALE_ROW0 = P - K // 32
RUN = BANK // 2
NEIGHBOURS = 8
CHUNKS = ((0, 256), (256, 256), (512, 256), (768, 128), (896, 64), (960, 64))
SCALAR_TAIL = 96
ROOT_S = 32.0
COPIED = 0


def tile_picked_inorm_none_p_kernel(tc, x_words, x_scales, w1, w2, gamma, offs, out):
    nc = tc.nc
    with ExitStack() as ctx:
        keep = ctx.enter_context(tc.tile_pool(name="keep", bufs=1))
        psum = ctx.enter_context(tc.psum_pool(name="psum", bufs=1))

        offsets = keep.tile([P, S // GROUP], U16, name="offsets")
        table_words = keep.tile([P, T], U32, name="table_words", align_bytes=64)
        table_scales = keep.tile([P, T], U8, name="table_scales", tag="scales_then_weights", align_bytes=64)
        w1_first = keep.tile([P, 2, H // 2], F32, name="w1_first")
        w1_second = keep.tile([P, 2, H // 2], F32, name="w1_second")
        w1_third = keep.tile([P, 2, H], F32, name="w1_third")
        x_codes = [keep.tile([P, BANK], U32, name=f"x_codes{s}", align_bytes=64) for s in range(HALVES)]
        picked_scales = keep.tile([P, S], U8, name="picked_scales", align_bytes=64)
        x_plane = keep.tile([P, S], U8, name="x_plane", align_bytes=64)

        nc.vector.memset(table_scales[0:SCALE_ROW0, :].bitcast(I32), 0)
        nc.vector.memset(x_plane[:].bitcast(I32), 0)

        nc.sync.dma_start(table_scales[SCALE_ROW0:P, :].bitcast(I32), x_scales[0].bitcast(I32))
        nc.sync.dma_start(offsets[:], offs)
        nc.sync.dma_start(table_words[:].bitcast(I32), x_words[0].rearrange("p n t -> p (n t)").bitcast(I32))
        w1_rows = w1.rearrange("(p j) c -> p j c", j=PACK)
        nc.sync.dma_start(w1_first[:], w1_rows[:, 0:2, 0 : H // 2])
        nc.sync.dma_start(w1_second[:], w1_rows[:, 0:2, H // 2 : H])
        nc.sync.dma_start(w1_third[:], w1_rows[:, 2:4, :])

        warm = keep.tile([P, 1], F32, name="warm")
        warm_out = keep.tile([P, 1], F32, name="warm_out")
        nc.vector.memset(warm[:], 1.0)
        nc.scalar.activation(warm_out[:], warm[:], ACT.Abs_reciprocal_sqrt)

        stats = {t: keep.tile([P, HALVES, 2, 3], F32, name=f"stats{t}", tag=f"stats{t}", align_bytes=64) for t in range(1, PACK)}

        terms = keep.tile([P, 3, PACK, 4], F32, name="terms")
        nc.vector.memset(terms[:, 0, 1:PACK, 0], -1.0)
        copy_terms = keep.tile([P, 2], F32, name="copy_terms")
        nc.vector.memset(copy_terms[:, 0:1], -float(S))

        nc.vector.tensor_copy(picked_scales[:], table_scales[:].indirect(offsets[:]))
        for q in range(P // QUADRANT):
            nc.sync.dma_start(
                x_plane[QUADRANT * q : QUADRANT * q + 4, :].bitcast(I32),
                picked_scales[SCALE_ROW0 + 4 * q : SCALE_ROW0 + 4 * q + 4, :].bitcast(I32),
            )
        late_weights = keep.tile([P, PACK * N + PACK], F32, name="late_weights", tag="scales_then_weights", align_bytes=64)
        w2_raw = late_weights[:, 0 : PACK * N].rearrange("p (t n) -> p t n", t=PACK)
        gain = late_weights[:, PACK * N :]
        nc.sync.dma_start(w2_raw, w2.rearrange("(p t) n -> p t n", t=PACK))
        nc.sync.dma_start(gain, gamma.rearrange("(p t) o -> p (t o)", t=PACK))
        for s in range(HALVES):
            nc.vector.tensor_copy(x_codes[s][:], table_words[:].indirect(offsets[:, s * BANK // GROUP : (s + 1) * BANK // GROUP]))

        h = {}
        for t in range(PACK):
            for s in range(HALVES):
                h[t, s] = psum.tile([P, BANK], F32, name=f"h{t}_{s}", tag=f"bank{HALVES * t + s}")

        def warm_tensor_engine(bank, passes):
            for w in range(passes):
                nc.tensor.matmul_mx(
                    out=bank[0:QUADRANT, :],
                    lhsT=x_codes[0][:, 0:QUADRANT].bitcast(FP8X4),
                    lhsT_scale=picked_scales[:, 0:QUADRANT],
                    rhs=x_codes[0][:].bitcast(FP8X4),
                    rhs_scale=picked_scales[:, 0:BANK],
                    start=True,
                    stop=True,
                )

        warm_tensor_engine(h[PACK - 1, HALVES - 1], 3)

        w1_bf = keep.tile([P, PACK, P, PACK], BF16, name="w1_bf", tag="dealt", align_bytes=64)

        def deal_w1(copy, raw, j0, m0, m1, t0, t1):
            src = raw.rearrange("p e (m t) -> p m e t", t=PACK)[:, :, :, t0:t1]
            dst = w1_bf[:].rearrange("p t m j -> p m j t")[:, m0:m1, j0 : j0 + 2, t0:t1]
            copy(dst, src)

        deal_w1(nc.scalar.copy, w1_first[:], 0, 0, P // 2, 0, PACK)
        deal_w1(nc.scalar.copy, w1_second[:], 0, P // 2, P, 0, PACK)
        deal_w1(nc.vector.tensor_copy, w1_third[:], 2, 0, P, 1, 2)
        deal_w1(nc.vector.tensor_copy, w1_third[:], 2, 0, P, 0, 1)
        deal_w1(nc.scalar.copy, w1_third[:], 2, 0, P, 2, 4)

        w1_codes = [keep.tile([P, P], U32, name=f"w1_codes{t}", align_bytes=64) for t in range(PACK)]
        w1_plane = [keep.tile([P, P], U8, name=f"w1_plane{t}", align_bytes=64) for t in range(PACK)]
        for t in (1, 0, 2, 3):
            nc.vector.quantize_mx(out=w1_codes[t][:].bitcast(FP8X4), scales=w1_plane[t][:], in_=w1_bf[:, t].rearrange("p m j -> p (m j)"))

        affine = {}

        def product(t, s):
            for c0 in range(0, BANK, RUN):
                nc.tensor.matmul_mx(
                    out=h[t, s][:, c0 : c0 + RUN],
                    lhsT=w1_codes[t][:].bitcast(FP8X4),
                    lhsT_scale=w1_plane[t][:],
                    rhs=x_codes[s][:, c0 : c0 + RUN].bitcast(FP8X4),
                    rhs_scale=x_plane[:, s * BANK + c0 : s * BANK + c0 + RUN],
                    start=True,
                    stop=True,
                )

        def stats_on_vector(t, s):
            nc.vector.bn_stats(stats[t][:, s].rearrange("p r e -> p (r e)"), h[t, s][:])

        def affine_of(t):
            nc.vector.bn_aggr(terms[:, 0, t, 1:3], stats[t][:].rearrange("p s r e -> p (s r e)"))
            tiles = slice(COPIED, t + 1, t - COPIED) if t == 2 else slice(t, t + 1)
            count = 2 if t == 2 else 1
            nc.scalar.activation(terms[:, 1, tiles, 0:2], terms[:, 0, tiles, 2:3].to_broadcast([P, count, 2]), ACT.Abs_reciprocal_sqrt, scale=1.0 / S, bias=EPS / S)
            affine[t] = keep.tile([P, 2], F32, name=f"affine{t}")
            if t == 1:
                nc.gpsimd.tensor_scalar(affine[t][:], terms[:, 0, t, 0:2], terms[:, 1, t, 0:1], terms[:, 2, t, 0:1], ALU.mult, ALU.mult)
            else:
                nc.vector.tensor_reduce(affine[t][:], terms[:, :, t, 0:2].rearrange("p f i -> p i f"), mybir.AxisListType.X, ALU.mult)

        def normalise_on_scalar(t, s):
            nc.scalar.activation(z_rows[s][:, t, :], h[t, s][:], ACT.Identity, bias=affine[t][:, 1:2], scale=affine[t][:, 0:1])

        def normalise_on_vector(t, s, c0, c1):
            nc.vector.tensor_scalar(z_rows[s][:, t, c0:c1], h[t, s][:, c0:c1], affine[t][:, 0:1], affine[t][:, 1:2], ALU.mult, ALU.add)

        for pair in ((1, COPIED), (2,), (3,)):
            for s in range(HALVES):
                for t in pair:
                    product(t, s)
        w2_bf = keep.tile([P, N, PACK], BF16, name="w2_bf", tag="dealt", align_bytes=64)
        nc.gpsimd.tensor_scalar(w2_bf[:], w2_raw.rearrange("p t n -> p n t"), 1.0, 0.0, ALU.mult, ALU.add)
        for s in range(HALVES):
            stats_on_vector(1, s)

        scaled_h = keep.tile([P, S], F32, name="scaled_h")
        part = keep.tile([P, HALVES], F32, name="part")
        mean_slot = keep.tile([P, 1], F32, name="minus_mean", tag="mean_then_rows", align_bytes=64)
        minus_mean = mean_slot[:]
        spent = keep.tile([P, S], BF16, name="spent")
        for s in range(HALVES):
            nc.scalar.activation(scaled_h[:, s * BANK : (s + 1) * BANK], h[COPIED, s][:], ACT.Identity, scale=-1.0 / (S * ROOT_S), accum_out=part[:, s : s + 1])
        nc.gpsimd.tensor_scalar(terms[:, 2, 1:PACK, 0:2], gain[:, 1:PACK].unsqueeze(2).to_broadcast([P, PACK - 1, 2]), -1.0 / ROOT_S, 0.0, ALU.mult, ALU.add)
        affine_of(1)
        nc.scalar.activation(minus_mean, part[:, 0:1], ACT.Identity, bias=part[:, 1:2], accum_out=copy_terms[:, 1:2])
        nc.scalar.activation(spent[:], scaled_h[:], ACT.Square, scale=-float(S), bias=minus_mean, accum_out=terms[:, 0, COPIED, 2:3])
        for s in range(HALVES):
            stats_on_vector(2, s)
        affine_of(2)
        z_all = keep.tile([P, HALVES, PACK, BANK], BF16, name="z_all", tag="mean_then_rows", align_bytes=64)
        z_rows = [z_all[:, s] for s in range(HALVES)]
        affine[COPIED] = keep.tile([P, 2], F32, name="copy_affine")
        nc.gpsimd.tensor_scalar(affine[COPIED][:], copy_terms[:], terms[:, 1, COPIED, 0:1], gain[:, COPIED : COPIED + 1], ALU.mult, ALU.mult)
        nc.gpsimd.tensor_scalar(z_all[:, :, COPIED, :], scaled_h[:].rearrange("p (s n) -> p s n", s=HALVES), affine[COPIED][:, 0:1], affine[COPIED][:, 1:2], ALU.mult, ALU.add)

        for s in range(HALVES):
            stats_on_vector(3, s)
        affine_of(3)

        w2_codes = keep.tile([P, N], U32, name="w2_codes", tag="stats2", align_bytes=64)
        w2_plane = keep.tile([P, N], U8, name="w2_plane", align_bytes=64)
        nc.vector.quantize_mx(out=w2_codes[:].bitcast(FP8X4), scales=w2_plane[:], in_=w2_bf[:].rearrange("p n t -> p (n t)"))

        for s in range(HALVES):
            normalise_on_scalar(1, s)
        for first, width in CHUNKS[:2]:
            normalise_on_vector(2, 0, first, first + width)
        normalise_on_scalar(2, 1)
        for first, width in CHUNKS[:2]:
            normalise_on_vector(3, 0, first, first + width)
        normalise_on_scalar(3, 1)

        z_bf = [keep.tile([P, width, PACK], BF16, name=f"z_bf{c}", align_bytes=64) for c, (first, width) in enumerate(CHUNKS)]

        def weave(copy, c, n0, n1):
            s, c0 = divmod(CHUNKS[c][0], BANK)
            copy(
                z_bf[c][:, n0:n1, :].rearrange("p (c i) t -> p c t i", i=NEIGHBOURS),
                z_rows[s][:, :, c0 + n0 : c0 + n1].rearrange("p t (c i) -> p c t i", i=NEIGHBOURS),
            )

        result = [keep.tile([P, RUN], F32, name=f"result{piece}") for piece in range(S // RUN)]

        products = {}

        def second_layer(c):
            first, width = CHUNKS[c]
            z_codes = keep.tile([P, width], U32, name=f"z_codes{c}", align_bytes=64)
            z_plane = keep.tile([P, width], U8, name=f"z_plane{c}", align_bytes=64)
            nc.vector.quantize_mx(out=z_codes[:].bitcast(FP8X4), scales=z_plane[:], in_=z_bf[c][:].rearrange("p n t -> p (n t)"))
            y = psum.tile([P, width], F32, name=f"y{c}", tag=f"bank{c}")
            nc.tensor.matmul_mx(
                out=y[:],
                lhsT=w2_codes[:].bitcast(FP8X4),
                lhsT_scale=w2_plane[:],
                rhs=z_codes[:].bitcast(FP8X4),
                rhs_scale=z_plane[:],
                start=True,
                stop=True,
            )
            products[c] = y

        def store(copy, c):
            first, width = CHUNKS[c]
            piece, c0 = divmod(first, RUN)
            copy(result[piece][:, c0 : c0 + width], products[c][:])
            if c0 + width == RUN:
                nc.sync.dma_start(out[:, piece * RUN : (piece + 1) * RUN], result[piece][:])

        last = len(CHUNKS) - 1
        for c in (1, 3, 4):
            weave(nc.scalar.copy, c, 0, CHUNKS[c][1])
        for c in (0, 2):
            weave(nc.vector.tensor_copy, c, 0, CHUNKS[c][1])
        for c in (0, 1, 2):
            second_layer(c)
        weave(nc.vector.tensor_copy, last, 0, CHUNKS[last][1])
        for c in range(3, len(CHUNKS)):
            second_layer(c)
        for c in range(len(CHUNKS)):
            store(nc.vector.tensor_copy if c > 2 else nc.scalar.copy, c)
